import numpy as np
import ml_dtypes


def mxq(x, axis, fmt="e4m3"):
    dtype, down = {"e4m3": (ml_dtypes.float8_e4m3fn, 7), "e5m2": (ml_dtypes.float8_e5m2, 14)}[fmt]
    v = np.moveaxis(np.asarray(x, np.float32).astype(ml_dtypes.bfloat16).astype(np.float64), axis, -1)
    blocks = v.reshape(v.shape[:-1] + (-1, 32))
    amax = np.abs(blocks).max(-1, keepdims=True)
    byte = np.maximum(np.where(amax > 0, np.frexp(amax)[1] - 1 + 127, 0) - down, 1)
    scale = np.exp2(byte - 127.0)
    codes = (blocks / scale).astype(np.float32).astype(dtype).astype(np.float64)
    return np.moveaxis((codes * scale).reshape(v.shape), -1, axis)


WIDE = False


def mx_kscale(k):
    if not WIDE:
        return np.ones(k)
    levels = np.array([10, -10, 5, -5, 0])
    if k % 512:
        return np.exp2(np.random.permutation(np.resize(levels, k // 32))).repeat(32)
    a = np.empty((k // 512, 16))
    for p in range(k // 512):
        a[p, :8] = np.random.permutation(np.resize(levels, 8))
        for g in range(8):
            far = levels[np.abs(levels - a[p, g]) >= 10]
            a[p, g + 8] = far[np.random.randint(len(far))]
    return np.exp2(a.ravel()).repeat(32)


def f64(x):
    return np.asarray(x).astype(np.float64)


def striped(idx):
    return np.tile(idx.reshape(-1, 16).T, (8, 1)).astype(np.uint16)


def unstriped(offs):
    return offs[:16].T.reshape(-1).astype(np.int64)


def pack_weight(w):
    k, n = w.shape
    w = f64(np.asarray(w, np.float32).astype(ml_dtypes.bfloat16)).reshape(k // 32, 32, n)
    amax = np.abs(w).max(1)
    byte = np.clip(np.where(amax > 0, np.frexp(amax)[1] - 1 + 127 - 7, 1), 1, 254)
    scaled = (w * np.exp2(127.0 - byte)[:, None, :]).reshape(k, n).astype(np.float32)
    words = np.ascontiguousarray(scaled.reshape(k // 512, 128, 4, n).transpose(0, 1, 3, 2)).astype(ml_dtypes.float8_e4m3fn).view(np.uint8)
    return words, np.ascontiguousarray(byte.astype(np.uint8).reshape(k // 512, 16, n))


def unpack_weight(words, scales):
    g, p, n, _ = words.shape
    vals = np.ascontiguousarray(words).view(ml_dtypes.float8_e4m3fn).astype(np.float64) * np.repeat(np.exp2(scales.astype(np.float64) - 127.0), 8, axis=1)[..., None]
    return vals.transpose(0, 1, 3, 2).reshape(g * 512, n)


def relu(v):
    return np.maximum(v, 0.0)


K, T, S, H, D, W, U = 512, 2048, 512, 512, 4, 2048, 512
P = 2 ** 7


def setup_inputs():
    n = np.random.standard_normal
    s = mx_kscale(K)[:, None]
    u = mx_kscale(H)
    packed_xT = pack_weight(n((K, T)) * s)
    packed_eT = pack_weight(n((H, W)) / np.sqrt(H) / u[:, None])
    return {
        "x_words": packed_xT[0],
        "x_scales": packed_xT[1],
        "w1": (n((K, H)) / np.sqrt(K) / s * u).astype(np.float32),
        "e_words": packed_eT[0],
        "e_scales": packed_eT[1],
        "nb": (np.tile(np.random.uniform(0.5, 1.5, W), (P, 1))).astype(np.float32),
        "own": (np.random.uniform(0.5, 1.5, (S, 1))).astype(np.float32),
        "offs": striped(np.random.permutation(T)[:S]),
        "oth": striped(np.random.permutation(W)[:U]),
    }


def reference(x_words, x_scales, w1, e_words, e_scales, nb, own, offs, oth):
    xq = unpack_weight(x_words, x_scales)[:, unstriped(offs)]
    h = mxq(f64(w1), 0, "e4m3").T @ xq
    e_oth = unpack_weight(e_words, e_scales)[:, unstriped(oth)]
    y = mxq(h, 0, "e4m3").T @ e_oth
    dd = f64(nb)[:1][:, unstriped(oth)] - y
    near = dd.reshape(len(dd), -1, D).min(axis=2)
    rr = near + f64(own)
    return np.sqrt(relu(rr) + 0.01)

@@ -1,0 +1,164 @@
+from contextlib import ExitStack
+
+import concourse.mybir as mybir
+from concourse.masks import make_identity
+
+K, T, S, H, D, W, U = 512, 2048, 512, 512, 4, 2048, 512
+P = 128
+V = U // D
+FLOPS = 2 * K * H * S + 2 * H * S * U
+
+F32 = mybir.dt.float32
+BF16 = mybir.dt.bfloat16
+I32 = mybir.dt.int32
+U32 = mybir.dt.uint32
+U16 = mybir.dt.uint16
+U8 = mybir.dt.uint8
+FP8X4 = mybir.dt.float8_e4m3fn_x4
+ALU = mybir.AluOpType
+ACT = mybir.ActivationFunctionType
+
+E_PLANE = 4
+NB_ROW = 8
+HALF = S // 2
+
+
+def tile_picked_ycham_root_p_kernel(tc, x_words, x_scales, w1, e_words, e_scales, nb, own, offs, oth, out):
+    nc = tc.nc
+    with ExitStack() as ctx:
+        keep = ctx.enter_context(tc.tile_pool(name="keep", bufs=1))
+        psum = ctx.enter_context(tc.psum_pool(name="psum", bufs=1))
+
+        def sb(name, shape, dtype):
+            return keep.tile(shape, dtype, name=name, align_bytes=64)
+
+        def bank(tag, name, shape):
+            return psum.tile(shape, F32, name=name, tag=tag)
+
+        offs_t = sb("offs_t", [P, S // 16], U16)
+        oth_t = sb("oth_t", [P, U // 16], U16)
+        xw = sb("xw", [P, T], I32)
+        ew = sb("ew", [P, W], I32)
+        xs = sb("xs", [P, T], U8)
+        es = sb("es", [P, W], U8)
+        nb_t = sb("nb_t", [P, W], F32)
+        own_t = sb("own_t", [P, 2, 2], F32)
+        w_raw = sb("w_raw", [P, 4, H], F32)
+        warm = sb("warm", [P, 1], F32)
+        ident = sb("ident", [P, P], F32)
+
+        nc.vector.memset(warm[:], 1.0)
+        nc.gpsimd.memset(xs[:].bitcast(I32), 0)
+        nc.gpsimd.memset(nb_t[:], 0.0)
+        nc.gpsimd.memset(es[:].bitcast(I32), 0)
+
+        nc.scalar.dma_start(w_raw[:], w1.rearrange("(p j) c -> p j c", j=4))
+        nc.sync.dma_start(offs_t[:], offs)
+        nc.sync.dma_start(oth_t[:], oth)
+        for q in range(4):
+            nc.sync.dma_start(xs[32 * q : 32 * q + 4, :].bitcast(I32), x_scales[0, 4 * q : 4 * q + 4, :].bitcast(I32))
+        warm_out = sb("warm_out", [P, 1], F32)
+        nc.scalar.activation(warm_out[:], warm[:], ACT.Sqrt)
+        nc.scalar.dma_start(xw[:], x_words[0].rearrange("p n t -> p (n t)").bitcast(I32))
+        nc.scalar.dma_start(ew[:], e_words[0].rearrange("p n t -> p (n t)").bitcast(I32))
+        nc.sync.dma_start(nb_t[NB_ROW : NB_ROW + 1, :], nb[0:1, :])
+        for q in range(4):
+            nc.sync.dma_start(es[32 * q + E_PLANE : 32 * q + E_PLANE + 4, :].bitcast(I32), e_scales[0, 4 * q : 4 * q + 4, :].bitcast(I32))
+        make_identity(nc, ident[:])
+        with nc.allow_non_contiguous_dma(reason="512 norms, two to a partition and half"):
+            nc.gpsimd.dma_start(own_t[:], own.rearrange("(h p a) o -> p h (a o)", h=2, a=2))
+
+        xg_s = sb("xg_s", [P, S], U8)
+        nc.vector.tensor_copy(xg_s[:], xs[:].indirect(offs_t[:]))
+        nb_g = sb("nb_g", [P, U], F32)
+        nc.vector.tensor_copy(nb_g[:], nb_t[:].indirect(oth_t[:]))
+
+        w_bf = sb("w_bf", [P, 4 * H], BF16)
+        w_codes = sb("w_codes", [P, H], U32)
+        w_sc = sb("w_sc", [P, H], U8)
+        w_dst = w_bf[:].rearrange("p (t m j) -> p m t j", t=4, j=4)
+        w_src = w_raw[:].rearrange("p j (m t) -> p m t j", t=4)
+        for u in range(2):
+            nc.scalar.copy(w_dst[:, :, 2 * u : 2 * u + 2, :], w_src[:, :, 2 * u : 2 * u + 2, :])
+        eg_s = sb("eg_s", [P, U], U8)
+        ep_s = sb("ep_s", [P, U], U8)
+        nc.vector.quantize_mx(out=w_codes[:, 0:256].bitcast(FP8X4), scales=w_sc[:, 0:256], in_=w_bf[:, 0:1024])
+        nc.vector.tensor_copy(eg_s[:], es[:].indirect(oth_t[:]))
+        nc.vector.quantize_mx(out=w_codes[:, 256:512].bitcast(FP8X4), scales=w_sc[:, 256:512], in_=w_bf[:, 1024:2048])
+
+        nb_ps = bank("y11", "nb_ps", [P, D, P])
+        for d in range(D):
+            nc.tensor.transpose(nb_ps[:, d, :], nb_g[:, d : U : D], ident[:])
+        neg_nb = sb("neg_nb", [P, D], F32)
+        nc.scalar.activation(neg_nb[:], nb_ps[:, :, NB_ROW], ACT.Copy, scale=-1.0)
+
+        xg_w = sb("xg_w", [P, S], U32)
+        for h in range(2):
+            nc.vector.tensor_copy(xg_w[:, h * HALF : (h + 1) * HALF], xw[:].bitcast(U32).indirect(offs_t[:, 16 * h : 16 * (h + 1)]))
+        nc.vector.tensor_copy(ep_s[:].rearrange("p (d v) -> p d v", d=D), eg_s[:].rearrange("p (v d) -> p d v", d=D))
+
+        h_bf = sb("h_bf", [P, 4 * S], BF16)
+        for g in range(4):
+            cols = slice(g * P, (g + 1) * P)
+            h_ps = bank("h%d" % g, "h_ps%d" % g, [P, 4, P])
+            for t in range(4):
+                nc.tensor.matmul_mx(
+                    out=h_ps[:, t, :],
+                    lhsT=w_codes[:, t * P : (t + 1) * P].bitcast(FP8X4),
+                    lhsT_scale=w_sc[:, t * P : (t + 1) * P],
+                    rhs=xg_w[:, cols].bitcast(FP8X4),
+                    rhs_scale=xg_s[:, cols],
+                    start=True,
+                    stop=True,
+                )
+            nc.scalar.copy(h_bf[:, 4 * g * P : 4 * (g + 1) * P].rearrange("p (n t) -> p n t", t=4), h_ps[:].rearrange("p t n -> p n t"))
+
+        ep_w = sb("ep_w", [P, U], U32)
+        nc.vector.tensor_copy(ep_w[:].rearrange("p (d v) -> p v d", d=D), ew[:].bitcast(U32).indirect(oth_t[:]))
+
+        h_codes = sb("h_codes", [P, S], U32)
+        h_sc = sb("h_sc", [P, S], U8)
+        for h in range(2):
+            cols = slice(h * HALF, (h + 1) * HALF)
+            nc.vector.quantize_mx(out=h_codes[:, cols].bitcast(FP8X4), scales=h_sc[:, cols], in_=h_bf[:, 4 * h * HALF : 4 * (h + 1) * HALF])
+
+        far = []
+        for h in range(2):
+            cols = slice(h * HALF, (h + 1) * HALF)
+            y_ps = [bank("y%d%d" % (h, e), "y_ps%d%d" % (h, e), [P, 2, HALF]) for e in range(2)]
+            for e in range(2):
+                for c in range(2):
+                    d = 2 * c + e
+                    nc.tensor.matmul_mx(
+                        out=y_ps[e][:, c, :],
+                        lhsT=ep_w[:, d * V : (d + 1) * V].bitcast(FP8X4),
+                        lhsT_scale=ep_s[E_PLANE:P, d * V : (d + 1) * V],
+                        rhs=h_codes[:, cols].bitcast(FP8X4),
+                        rhs_scale=h_sc[:, cols],
+                        start=True,
+                        stop=True,
+                    )
+            pair = []
+            for c in range(2):
+                even = sb("even%d%d" % (h, c), [P, 2, P], F32)
+                nc.scalar.activation(even[:], y_ps[0][:, c, :].rearrange("p (n a) -> p a n", a=2), ACT.Identity, bias=neg_nb[:, 2 * c : 2 * c + 1])
+                both = sb("both%d%d" % (h, c), [P, 2, P], F32)
+                nc.vector.scalar_tensor_tensor(
+                    both[:], y_ps[1][:, c, :].rearrange("p (n a) -> p a n", a=2), neg_nb[:, 2 * c + 1 : 2 * c + 2], even[:], ALU.add, ALU.max
+                )
+                pair.append(both)
+            top = sb("top%d" % h, [P, 2, P], F32)
+            for a in range(2):
+                nc.vector.tensor_tensor(top[:, a, :], pair[0][:, a, :], pair[1][:, a, :], ALU.max)
+            far.append(top)
+
+        for h in range(2):
+            rr = sb("rr%d" % h, [P, 2, V], F32)
+            res = sb("res%d" % h, [P, 2, V], F32)
+            for a in range(2):
+                o_ps = bank("h%d" % (2 * h + a), "o_ps%d%d" % (h, a), [P, V])
+                nc.tensor.transpose(o_ps[:], far[h][:, a, :], ident[:])
+                nc.scalar.activation(rr[:, a, :], o_ps[:], ACT.Relu, bias=own_t[:, h, a : a + 1], scale=-1.0)
+            for a in range(2):
+                nc.scalar.activation(res[:, a, :], rr[:, a, :], ACT.Sqrt, bias=0.01)
+            nc.sync.dma_start(out[h * HALF : (h + 1) * HALF, :].rearrange("(p a) v -> p a v", a=2), res[:])

@@ -29,44 +29,41 @@ def tile_picked_ycham_root_p_kernel(tc, x_words, x_scales, w1, e_words, e_scales
         keep = ctx.enter_context(tc.tile_pool(name="keep", bufs=1))
         psum = ctx.enter_context(tc.psum_pool(name="psum", bufs=1))
 
-        def sb(name, shape, dtype):
-            return keep.tile(shape, dtype, name=name, align_bytes=64)
+        def sb(name, shape, dtype, tag=None):
+            return keep.tile(shape, dtype, name=name, tag=tag or name, align_bytes=64)
 
         def bank(tag, name, shape):
             return psum.tile(shape, F32, name=name, tag=tag)
 
         offs_t = sb("offs_t", [P, S // 16], U16)
         oth_t = sb("oth_t", [P, U // 16], U16)
-        xw = sb("xw", [P, T], I32)
-        ew = sb("ew", [P, W], I32)
         xs = sb("xs", [P, T], U8)
         es = sb("es", [P, W], U8)
         nb_t = sb("nb_t", [P, W], F32)
-        own_t = sb("own_t", [P, 2, 2], F32)
         w_raw = sb("w_raw", [P, 4, H], F32)
         warm = sb("warm", [P, 1], F32)
+        warm_out = sb("warm_out", [P, 1], F32)
         ident = sb("ident", [P, P], F32)
 
         nc.vector.memset(warm[:], 1.0)
-        nc.gpsimd.memset(xs[:].bitcast(I32), 0)
-        nc.gpsimd.memset(nb_t[:], 0.0)
-        nc.gpsimd.memset(es[:].bitcast(I32), 0)
+        nc.vector.memset(xs[:].bitcast(I32), 0)
+        nc.vector.memset(nb_t[:], 0.0)
+        nc.vector.memset(es[:].bitcast(I32), 0)
 
         nc.scalar.dma_start(w_raw[:], w1.rearrange("(p j) c -> p j c", j=4))
         nc.sync.dma_start(offs_t[:], offs)
         nc.sync.dma_start(oth_t[:], oth)
         for q in range(4):
             nc.sync.dma_start(xs[32 * q : 32 * q + 4, :].bitcast(I32), x_scales[0, 4 * q : 4 * q + 4, :].bitcast(I32))
-        warm_out = sb("warm_out", [P, 1], F32)
         nc.scalar.activation(warm_out[:], warm[:], ACT.Sqrt)
+        xw = sb("xw", [P, T], I32, tag="warm_out")
         nc.scalar.dma_start(xw[:], x_words[0].rearrange("p n t -> p (n t)").bitcast(I32))
+        ew = sb("ew", [P, W], I32, tag="warm")
         nc.scalar.dma_start(ew[:], e_words[0].rearrange("p n t -> p (n t)").bitcast(I32))
         nc.sync.dma_start(nb_t[NB_ROW : NB_ROW + 1, :], nb[0:1, :])
         for q in range(4):
             nc.sync.dma_start(es[32 * q + E_PLANE : 32 * q + E_PLANE + 4, :].bitcast(I32), e_scales[0, 4 * q : 4 * q + 4, :].bitcast(I32))
         make_identity(nc, ident[:])
-        with nc.allow_non_contiguous_dma(reason="512 norms, two to a partition and half"):
-            nc.gpsimd.dma_start(own_t[:], own.rearrange("(h p a) o -> p h (a o)", h=2, a=2))
 
         xg_s = sb("xg_s", [P, S], U8)
         nc.vector.tensor_copy(xg_s[:], xs[:].indirect(offs_t[:]))
@@ -84,6 +81,9 @@ def tile_picked_ycham_root_p_kernel(tc, x_words, x_scales, w1, e_words, e_scales
         ep_s = sb("ep_s", [P, U], U8)
         nc.vector.quantize_mx(out=w_codes[:, 0:256].bitcast(FP8X4), scales=w_sc[:, 0:256], in_=w_bf[:, 0:1024])
         nc.vector.tensor_copy(eg_s[:], es[:].indirect(oth_t[:]))
+        own_t = sb("own_t", [P, 2, 2], F32, tag="nb_t")
+        with nc.allow_non_contiguous_dma(reason="512 norms, two to a partition and half"):
+            nc.sync.dma_start(own_t[:], own.rearrange("(h p a) o -> p h (a o)", h=2, a=2))
         nc.vector.quantize_mx(out=w_codes[:, 256:512].bitcast(FP8X4), scales=w_sc[:, 256:512], in_=w_bf[:, 1024:2048])
 
         nb_ps = bank("y11", "nb_ps", [P, D, P])
@@ -92,9 +92,10 @@ def tile_picked_ycham_root_p_kernel(tc, x_words, x_scales, w1, e_words, e_scales
         neg_nb = sb("neg_nb", [P, D], F32)
         nc.scalar.activation(neg_nb[:], nb_ps[:, :, NB_ROW], ACT.Copy, scale=-1.0)
 
-        xg_w = sb("xg_w", [P, S], U32)
-        for h in range(2):
-            nc.vector.tensor_copy(xg_w[:, h * HALF : (h + 1) * HALF], xw[:].bitcast(U32).indirect(offs_t[:, 16 * h : 16 * (h + 1)]))
+        xg_w = []
+        for h, tag in enumerate(("es", "w_bf")):
+            xg_w.append(sb("xg_w%d" % h, [P, HALF], U32, tag=tag))
+            nc.vector.tensor_copy(xg_w[h][:], xw[:].bitcast(U32).indirect(offs_t[:, 16 * h : 16 * (h + 1)]))
         nc.vector.tensor_copy(ep_s[:].rearrange("p (d v) -> p d v", d=D), eg_s[:].rearrange("p (v d) -> p d v", d=D))
 
         h_bf = sb("h_bf", [P, 4 * S], BF16)
@@ -106,14 +107,14 @@ def tile_picked_ycham_root_p_kernel(tc, x_words, x_scales, w1, e_words, e_scales
                     out=h_ps[:, t, :],
                     lhsT=w_codes[:, t * P : (t + 1) * P].bitcast(FP8X4),
                     lhsT_scale=w_sc[:, t * P : (t + 1) * P],
-                    rhs=xg_w[:, cols].bitcast(FP8X4),
+                    rhs=xg_w[g // 2][:, (g % 2) * P : (g % 2 + 1) * P].bitcast(FP8X4),
                     rhs_scale=xg_s[:, cols],
                     start=True,
                     stop=True,
                 )
             nc.scalar.copy(h_bf[:, 4 * g * P : 4 * (g + 1) * P].rearrange("p (n t) -> p n t", t=4), h_ps[:].rearrange("p t n -> p n t"))
 
-        ep_w = sb("ep_w", [P, U], U32)
+        ep_w = sb("ep_w", [P, U], U32, tag="warm_out")
         nc.vector.tensor_copy(ep_w[:].rearrange("p (d v) -> p v d", d=D), ew[:].bitcast(U32).indirect(oth_t[:]))
 
         h_codes = sb("h_codes", [P, S], U32)

@@ -45,58 +45,52 @@ def tile_picked_ycham_root_p_kernel(tc, x_words, x_scales, w1, e_words, e_scales
         warm_out = sb("warm_out", [P, 1], F32)
         ident = sb("ident", [P, P], F32)
 
-        nc.vector.memset(warm[:], 1.0)
+        own_t = sb("own_t", [P, 2, 2], F32)
+        make_identity(nc, ident[:])
+        nc.vector.memset(es[:].bitcast(I32), 0)
         nc.vector.memset(xs[:].bitcast(I32), 0)
         nc.vector.memset(nb_t[:], 0.0)
-        nc.vector.memset(es[:].bitcast(I32), 0)
+        nc.vector.memset(warm[:], 1.0)
 
-        nc.scalar.dma_start(w_raw[:], w1.rearrange("(p j) c -> p j c", j=4))
         nc.sync.dma_start(offs_t[:], offs)
         nc.sync.dma_start(oth_t[:], oth)
-        for q in range(4):
-            nc.sync.dma_start(xs[32 * q : 32 * q + 4, :].bitcast(I32), x_scales[0, 4 * q : 4 * q + 4, :].bitcast(I32))
-        nc.scalar.activation(warm_out[:], warm[:], ACT.Sqrt)
-        xw = sb("xw", [P, T], I32, tag="warm_out")
-        nc.scalar.dma_start(xw[:], x_words[0].rearrange("p n t -> p (n t)").bitcast(I32))
-        ew = sb("ew", [P, W], I32, tag="warm")
-        nc.scalar.dma_start(ew[:], e_words[0].rearrange("p n t -> p (n t)").bitcast(I32))
-        nc.sync.dma_start(nb_t[NB_ROW : NB_ROW + 1, :], nb[0:1, :])
+        with nc.allow_non_contiguous_dma(reason="512 norms, two to a partition and half"):
+            nc.sync.dma_start(own_t[:], own.rearrange("(h p a) o -> p h (a o)", h=2, a=2))
         for q in range(4):
             nc.sync.dma_start(es[32 * q + E_PLANE : 32 * q + E_PLANE + 4, :].bitcast(I32), e_scales[0, 4 * q : 4 * q + 4, :].bitcast(I32))
-        make_identity(nc, ident[:])
+        nc.sync.dma_start(w_raw[:], w1.rearrange("(p j) c -> p j c", j=4))
+        for q in range(4):
+            nc.sync.dma_start(xs[32 * q : 32 * q + 4, :].bitcast(I32), x_scales[0, 4 * q : 4 * q + 4, :].bitcast(I32))
+        nc.sync.dma_start(nb_t[NB_ROW : NB_ROW + 1, :], nb[0:1, :])
+        nc.scalar.activation(warm_out[:], warm[:], ACT.Sqrt)
+        xw = sb("xw", [P, T], I32, tag="warm")
+        nc.sync.dma_start(xw[:], x_words[0].rearrange("p n t -> p (n t)").bitcast(I32))
+        ew = sb("ew", [P, W], I32, tag="warm_out")
+        nc.sync.dma_start(ew[:], e_words[0].rearrange("p n t -> p (n t)").bitcast(I32))
 
+        eg_s = sb("eg_s", [P, U], U8)
+        ep_s = sb("ep_s", [P, U], U8)
+        nc.vector.tensor_copy(eg_s[:], es[:].indirect(oth_t[:]))
+        nc.vector.tensor_copy(ep_s[:].rearrange("p (d v) -> p d v", d=D), eg_s[:].rearrange("p (v d) -> p d v", d=D))
         xg_s = sb("xg_s", [P, S], U8)
         nc.vector.tensor_copy(xg_s[:], xs[:].indirect(offs_t[:]))
-        nb_g = sb("nb_g", [P, U], F32)
-        nc.vector.tensor_copy(nb_g[:], nb_t[:].indirect(oth_t[:]))
 
         w_bf = sb("w_bf", [P, 4 * H], BF16)
-        w_codes = sb("w_codes", [P, H], U32)
+        w_codes = sb("w_codes", [P, H], U32, tag="xs")
         w_sc = sb("w_sc", [P, H], U8)
         w_dst = w_bf[:].rearrange("p (t m j) -> p m t j", t=4, j=4)
         w_src = w_raw[:].rearrange("p j (m t) -> p m t j", t=4)
-        for u in range(2):
-            nc.scalar.copy(w_dst[:, :, 2 * u : 2 * u + 2, :], w_src[:, :, 2 * u : 2 * u + 2, :])
-        eg_s = sb("eg_s", [P, U], U8)
-        ep_s = sb("ep_s", [P, U], U8)
-        nc.vector.quantize_mx(out=w_codes[:, 0:256].bitcast(FP8X4), scales=w_sc[:, 0:256], in_=w_bf[:, 0:1024])
-        nc.vector.tensor_copy(eg_s[:], es[:].indirect(oth_t[:]))
-        own_t = sb("own_t", [P, 2, 2], F32, tag="nb_t")
-        with nc.allow_non_contiguous_dma(reason="512 norms, two to a partition and half"):
-            nc.sync.dma_start(own_t[:], own.rearrange("(h p a) o -> p h (a o)", h=2, a=2))
-        nc.vector.quantize_mx(out=w_codes[:, 256:512].bitcast(FP8X4), scales=w_sc[:, 256:512], in_=w_bf[:, 1024:2048])
-
-        nb_ps = bank("y11", "nb_ps", [P, D, P])
-        for d in range(D):
-            nc.tensor.transpose(nb_ps[:, d, :], nb_g[:, d : U : D], ident[:])
-        neg_nb = sb("neg_nb", [P, D], F32)
-        nc.scalar.activation(neg_nb[:], nb_ps[:, :, NB_ROW], ACT.Copy, scale=-1.0)
+        nc.scalar.copy(w_dst[:, :, 0:2, :], w_src[:, :, 0:2, :])
+        nc.vector.tensor_copy(w_dst[:, :, 2:4, :], w_src[:, :, 2:4, :])
+        nc.vector.quantize_mx(out=w_codes[:].bitcast(FP8X4), scales=w_sc[:], in_=w_bf[:])
 
         xg_w = []
-        for h, tag in enumerate(("es", "w_bf")):
+        for h, tag in enumerate(("w_bf", "xg_w1")):
             xg_w.append(sb("xg_w%d" % h, [P, HALF], U32, tag=tag))
             nc.vector.tensor_copy(xg_w[h][:], xw[:].bitcast(U32).indirect(offs_t[:, 16 * h : 16 * (h + 1)]))
-        nc.vector.tensor_copy(ep_s[:].rearrange("p (d v) -> p d v", d=D), eg_s[:].rearrange("p (v d) -> p d v", d=D))
+
+        nb_g = sb("nb_g", [P, U], F32, tag="warm")
+        nc.vector.tensor_copy(nb_g[:], nb_t[:].indirect(oth_t[:]))
 
         h_bf = sb("h_bf", [P, 4 * S], BF16)
         for g in range(4):
@@ -114,7 +108,13 @@ def tile_picked_ycham_root_p_kernel(tc, x_words, x_scales, w1, e_words, e_scales
                 )
             nc.scalar.copy(h_bf[:, 4 * g * P : 4 * (g + 1) * P].rearrange("p (n t) -> p n t", t=4), h_ps[:].rearrange("p t n -> p n t"))
 
-        ep_w = sb("ep_w", [P, U], U32, tag="warm_out")
+        nb_ps = bank("y11", "nb_ps", [P, D, P])
+        for d in range(D):
+            nc.tensor.transpose(nb_ps[:, d, :], nb_g[:, d : U : D], ident[:])
+        neg_nb = sb("neg_nb", [P, D], F32)
+        nc.scalar.activation(neg_nb[:], nb_ps[:, :, NB_ROW], ACT.Copy, scale=-1.0)
+
+        ep_w = sb("ep_w", [P, U], U32)
         nc.vector.tensor_copy(ep_w[:].rearrange("p (d v) -> p v d", d=D), ew[:].bitcast(U32).indirect(oth_t[:]))
 
         h_codes = sb("h_codes", [P, S], U32)
@@ -127,30 +127,23 @@ def tile_picked_ycham_root_p_kernel(tc, x_words, x_scales, w1, e_words, e_scales
         for h in range(2):
             cols = slice(h * HALF, (h + 1) * HALF)
             y_ps = [bank("y%d%d" % (h, e), "y_ps%d%d" % (h, e), [P, 2, HALF]) for e in range(2)]
-            for e in range(2):
-                for c in range(2):
-                    d = 2 * c + e
-                    nc.tensor.matmul_mx(
-                        out=y_ps[e][:, c, :],
-                        lhsT=ep_w[:, d * V : (d + 1) * V].bitcast(FP8X4),
-                        lhsT_scale=ep_s[E_PLANE:P, d * V : (d + 1) * V],
-                        rhs=h_codes[:, cols].bitcast(FP8X4),
-                        rhs_scale=h_sc[:, cols],
-                        start=True,
-                        stop=True,
-                    )
-            pair = []
-            for c in range(2):
-                even = sb("even%d%d" % (h, c), [P, 2, P], F32)
-                nc.scalar.activation(even[:], y_ps[0][:, c, :].rearrange("p (n a) -> p a n", a=2), ACT.Identity, bias=neg_nb[:, 2 * c : 2 * c + 1])
-                both = sb("both%d%d" % (h, c), [P, 2, P], F32)
-                nc.vector.scalar_tensor_tensor(
-                    both[:], y_ps[1][:, c, :].rearrange("p (n a) -> p a n", a=2), neg_nb[:, 2 * c + 1 : 2 * c + 2], even[:], ALU.add, ALU.max
+            for d in range(D):
+                nc.tensor.matmul_mx(
+                    out=y_ps[d // 2][:, d % 2, :],
+                    lhsT=ep_w[:, d * V : (d + 1) * V].bitcast(FP8X4),
+                    lhsT_scale=ep_s[E_PLANE:P, d * V : (d + 1) * V],
+                    rhs=h_codes[:, cols].bitcast(FP8X4),
+                    rhs_scale=h_sc[:, cols],
+                    start=True,
+                    stop=True,
                 )
-                pair.append(both)
-            top = sb("top%d" % h, [P, 2, P], F32)
-            for a in range(2):
-                nc.vector.tensor_tensor(top[:, a, :], pair[0][:, a, :], pair[1][:, a, :], ALU.max)
+            y = [y_ps[d // 2][:, d % 2, :].rearrange("p (n a) -> p a n", a=2) for d in range(D)]
+            top = sb("top%d0" % h, [P, 2, P], F32)
+            nc.scalar.activation(top[:], y[0], ACT.Identity, bias=neg_nb[:, 0:1])
+            for d in range(1, D):
+                last, top = top, sb("top%d%d" % (h, d), [P, 2, P], F32)
+                for part in [slice(0, 2)] if d < D - 1 else [slice(0, 1), slice(1, 2)]:
+                    nc.vector.scalar_tensor_tensor(top[:, part, :], y[d][:, part, :], neg_nb[:, d : d + 1], last[:, part, :], ALU.add, ALU.max)
             far.append(top)
 
         for h in range(2):
@@ -159,7 +152,9 @@ def tile_picked_ycham_root_p_kernel(tc, x_words, x_scales, w1, e_words, e_scales
             for a in range(2):
                 o_ps = bank("h%d" % (2 * h + a), "o_ps%d%d" % (h, a), [P, V])
                 nc.tensor.transpose(o_ps[:], far[h][:, a, :], ident[:])
-                nc.scalar.activation(rr[:, a, :], o_ps[:], ACT.Relu, bias=own_t[:, h, a : a + 1], scale=-1.0)
-            for a in range(2):
-                nc.scalar.activation(res[:, a, :], rr[:, a, :], ACT.Sqrt, bias=0.01)
+                if h == 0:
+                    nc.scalar.activation(rr[:, a, :], o_ps[:], ACT.Relu, bias=own_t[:, h, a : a + 1], scale=-1.0)
+                else:
+                    nc.vector.tensor_scalar(rr[:, a, :], o_ps[:], own_t[:, h, a : a + 1], 0.0, ALU.subtract, ALU.min)
+            nc.scalar.activation(res[:], rr[:], ACT.Sqrt, bias=0.01, scale=1.0 if h == 0 else -1.0)
             nc.sync.dma_start(out[h * HALF : (h + 1) * HALF, :].rearrange("(p a) v -> p a v", a=2), res[:])

@@ -19,8 +19,10 @@ ALU = mybir.AluOpType
 ACT = mybir.ActivationFunctionType
 
 E_PLANE = 4
-NB_ROW = 8
+NB_ROW = P - 1
 HALF = S // 2
+M_SCALAR = 96
+NB_VECTOR = 3 * W // 4
 
 
 def tile_picked_ycham_root_p_kernel(tc, x_words, x_scales, w1, e_words, e_scales, nb, own, offs, oth, out):
@@ -32,70 +34,83 @@ def tile_picked_ycham_root_p_kernel(tc, x_words, x_scales, w1, e_words, e_scales
         def sb(name, shape, dtype, tag=None):
             return keep.tile(shape, dtype, name=name, tag=tag or name, align_bytes=64)
 
-        def bank(tag, name, shape):
-            return psum.tile(shape, F32, name=name, tag=tag)
+        def bank(b, name, shape):
+            return psum.tile(shape, F32, name=name, tag="bank%d" % b)
 
         offs_t = sb("offs_t", [P, S // 16], U16)
         oth_t = sb("oth_t", [P, U // 16], U16)
-        xs = sb("xs", [P, T], U8)
         es = sb("es", [P, W], U8)
         nb_t = sb("nb_t", [P, W], F32)
         w_raw = sb("w_raw", [P, 4, H], F32)
-        warm = sb("warm", [P, 1], F32)
-        warm_out = sb("warm_out", [P, 1], F32)
-        ident = sb("ident", [P, P], F32)
+        eps = sb("eps", [P, 1], F32)
+        own_t = sb("own_t", [P, 4], F32)
+        one = sb("one", [P, 1], F32)
+        xs = sb("xs", [P, T], U8)
+        xw = sb("xw", [P, T], I32)
+        ew = sb("ew", [P, W], I32)
 
-        own_t = sb("own_t", [P, 2, 2], F32)
-        make_identity(nc, ident[:])
         nc.vector.memset(es[:].bitcast(I32), 0)
         nc.vector.memset(xs[:].bitcast(I32), 0)
-        nc.vector.memset(nb_t[:], 0.0)
-        nc.vector.memset(warm[:], 1.0)
+        nc.vector.memset(one[:], 1.0)
+        nc.vector.memset(nb_t[0:NB_ROW, 0:NB_VECTOR], 0.0)
+        nc.scalar.activation(eps[:], one[:], ACT.Sqrt, scale=1e-4)
+        nc.scalar.activation(nb_t[0:NB_ROW, NB_VECTOR:W], eps[0:NB_ROW, :].to_broadcast([NB_ROW, W - NB_VECTOR]), ACT.Copy, scale=0.0)
+        ident = sb("ident", [P, P], F32, tag="one")
+        make_identity(nc, ident[:])
+        w_rows = w1.rearrange("(p j) c -> p j c", j=4)
 
-        nc.sync.dma_start(offs_t[:], offs)
         nc.sync.dma_start(oth_t[:], oth)
-        with nc.allow_non_contiguous_dma(reason="512 norms, two to a partition and half"):
-            nc.sync.dma_start(own_t[:], own.rearrange("(h p a) o -> p h (a o)", h=2, a=2))
+        nc.sync.dma_start(nb_t[NB_ROW : NB_ROW + 1, :], nb[0:1, :])
+        nc.sync.dma_start(w_raw[:, 0:1, :], w_rows[:, 0:1, :])
         for q in range(4):
             nc.sync.dma_start(es[32 * q + E_PLANE : 32 * q + E_PLANE + 4, :].bitcast(I32), e_scales[0, 4 * q : 4 * q + 4, :].bitcast(I32))
-        nc.sync.dma_start(w_raw[:], w1.rearrange("(p j) c -> p j c", j=4))
+        nc.sync.dma_start(w_raw[:, 1:4, :], w_rows[:, 1:4, :])
+        nc.sync.dma_start(offs_t[:], offs)
         for q in range(4):
             nc.sync.dma_start(xs[32 * q : 32 * q + 4, :].bitcast(I32), x_scales[0, 4 * q : 4 * q + 4, :].bitcast(I32))
-        nc.sync.dma_start(nb_t[NB_ROW : NB_ROW + 1, :], nb[0:1, :])
-        nc.scalar.activation(warm_out[:], warm[:], ACT.Sqrt)
-        xw = sb("xw", [P, T], I32, tag="warm")
         nc.sync.dma_start(xw[:], x_words[0].rearrange("p n t -> p (n t)").bitcast(I32))
-        ew = sb("ew", [P, W], I32, tag="warm_out")
         nc.sync.dma_start(ew[:], e_words[0].rearrange("p n t -> p (n t)").bitcast(I32))
+        with nc.allow_non_contiguous_dma(reason="512 norms, two to a partition and half"):
+            nc.sync.dma_start(own_t[:], own.rearrange("(g p) o -> p (g o)", g=4))
 
         eg_s = sb("eg_s", [P, U], U8)
-        ep_s = sb("ep_s", [P, U], U8)
         nc.vector.tensor_copy(eg_s[:], es[:].indirect(oth_t[:]))
-        nc.vector.tensor_copy(ep_s[:].rearrange("p (d v) -> p d v", d=D), eg_s[:].rearrange("p (v d) -> p d v", d=D))
+        nb_g = sb("nb_g", [P, U], F32)
+        nc.vector.tensor_copy(nb_g[:], nb_t[:].indirect(oth_t[:]))
+
+        w_bf = sb("w_bf", [P, 4 * H], BF16)
+        w_dst = w_bf[:].rearrange("p (t m j) -> p m t j", t=4, j=4)
+        w_src = w_raw[:].rearrange("p j (m t) -> p m t j", t=4)
+        nc.scalar.copy(w_dst[:, 0:M_SCALAR], w_src[:, 0:M_SCALAR])
+        nc.vector.tensor_copy(w_dst[:, M_SCALAR:P], w_src[:, M_SCALAR:P])
+
         xg_s = sb("xg_s", [P, S], U8)
         nc.vector.tensor_copy(xg_s[:], xs[:].indirect(offs_t[:]))
 
-        w_bf = sb("w_bf", [P, 4 * H], BF16)
         w_codes = sb("w_codes", [P, H], U32, tag="xs")
         w_sc = sb("w_sc", [P, H], U8)
-        w_dst = w_bf[:].rearrange("p (t m j) -> p m t j", t=4, j=4)
-        w_src = w_raw[:].rearrange("p j (m t) -> p m t j", t=4)
-        nc.scalar.copy(w_dst[:, :, 0:2, :], w_src[:, :, 0:2, :])
-        nc.vector.tensor_copy(w_dst[:, :, 2:4, :], w_src[:, :, 2:4, :])
         nc.vector.quantize_mx(out=w_codes[:].bitcast(FP8X4), scales=w_sc[:], in_=w_bf[:])
 
+        nb_ps = bank(7, "nb_ps", [P, D, P])
+        for d in range(D):
+            nc.tensor.transpose(nb_ps[:, d, :], nb_g[:, d : U : D], ident[:])
+        neg_nb = sb("neg_nb", [P, D], F32, tag="w_raw")
+        nc.scalar.activation(neg_nb[:], nb_ps[:, :, NB_ROW], ACT.Copy, scale=-1.0)
+
         xg_w = []
-        for h, tag in enumerate(("w_bf", "xg_w1")):
-            xg_w.append(sb("xg_w%d" % h, [P, HALF], U32, tag=tag))
+        for h in range(2):
+            xg_w.append(sb("xg_w%d" % h, [P, HALF], U32))
             nc.vector.tensor_copy(xg_w[h][:], xw[:].bitcast(U32).indirect(offs_t[:, 16 * h : 16 * (h + 1)]))
 
-        nb_g = sb("nb_g", [P, U], F32, tag="warm")
-        nc.vector.tensor_copy(nb_g[:], nb_t[:].indirect(oth_t[:]))
+        ep_s = sb("ep_s", [P, U], U8, tag="xw")
+        nc.vector.tensor_copy(ep_s[:].rearrange("p (d v) -> p d v", d=D), eg_s[:].rearrange("p (v d) -> p d v", d=D))
 
-        h_bf = sb("h_bf", [P, 4 * S], BF16)
+        pieces = [(0, 2), (2, 1), (3, 1)]
+        piece_of = [0, 0, 1, 2]
+        h_bf = [sb("h_bf%d" % i, [P, 4 * n * P], BF16) for i, (g0, n) in enumerate(pieces)]
         for g in range(4):
             cols = slice(g * P, (g + 1) * P)
-            h_ps = bank("h%d" % g, "h_ps%d" % g, [P, 4, P])
+            h_ps = bank(g, "h_ps%d" % g, [P, 4, P])
             for t in range(4):
                 nc.tensor.matmul_mx(
                     out=h_ps[:, t, :],
@@ -106,55 +121,55 @@ def tile_picked_ycham_root_p_kernel(tc, x_words, x_scales, w1, e_words, e_scales
                     start=True,
                     stop=True,
                 )
-            nc.scalar.copy(h_bf[:, 4 * g * P : 4 * (g + 1) * P].rearrange("p (n t) -> p n t", t=4), h_ps[:].rearrange("p t n -> p n t"))
-
-        nb_ps = bank("y11", "nb_ps", [P, D, P])
-        for d in range(D):
-            nc.tensor.transpose(nb_ps[:, d, :], nb_g[:, d : U : D], ident[:])
-        neg_nb = sb("neg_nb", [P, D], F32)
-        nc.scalar.activation(neg_nb[:], nb_ps[:, :, NB_ROW], ACT.Copy, scale=-1.0)
+            g_in = g - pieces[piece_of[g]][0]
+            nc.scalar.copy(h_bf[piece_of[g]][:, 4 * g_in * P : 4 * (g_in + 1) * P].rearrange("p (n t) -> p n t", t=4), h_ps[:].rearrange("p t n -> p n t"))
 
         ep_w = sb("ep_w", [P, U], U32)
         nc.vector.tensor_copy(ep_w[:].rearrange("p (d v) -> p v d", d=D), ew[:].bitcast(U32).indirect(oth_t[:]))
 
-        h_codes = sb("h_codes", [P, S], U32)
-        h_sc = sb("h_sc", [P, S], U8)
-        for h in range(2):
-            cols = slice(h * HALF, (h + 1) * HALF)
-            nc.vector.quantize_mx(out=h_codes[:, cols].bitcast(FP8X4), scales=h_sc[:, cols], in_=h_bf[:, 4 * h * HALF : 4 * (h + 1) * HALF])
-
-        far = []
-        for h in range(2):
-            cols = slice(h * HALF, (h + 1) * HALF)
-            y_ps = [bank("y%d%d" % (h, e), "y_ps%d%d" % (h, e), [P, 2, HALF]) for e in range(2)]
+        y = {}
+        for i, (g0, n) in enumerate(pieces):
+            h_codes = sb("h_codes%d" % i, [P, n * P], U32, tag="ew" if i == 0 else None)
+            h_sc = sb("h_sc%d" % i, [P, n * P], U8)
+            nc.vector.quantize_mx(out=h_codes[:].bitcast(FP8X4), scales=h_sc[:], in_=h_bf[i][:])
+            if n == 2:
+                for d in range(D):
+                    y[i, d] = bank(4 + d, "y_ps%d%d" % (i, d), [P, n * P])[:]
+            else:
+                y[i, 0] = bank(2 * i - 2, "y_first%d" % i, [P, P])[:]
+                rest = bank(2 * i - 1, "y_rest%d" % i, [P, D - 1, P])
+                for d in range(1, D):
+                    y[i, d] = rest[:, d - 1, :]
             for d in range(D):
                 nc.tensor.matmul_mx(
-                    out=y_ps[d // 2][:, d % 2, :],
+                    out=y[i, d],
                     lhsT=ep_w[:, d * V : (d + 1) * V].bitcast(FP8X4),
                     lhsT_scale=ep_s[E_PLANE:P, d * V : (d + 1) * V],
-                    rhs=h_codes[:, cols].bitcast(FP8X4),
-                    rhs_scale=h_sc[:, cols],
+                    rhs=h_codes[:].bitcast(FP8X4),
+                    rhs_scale=h_sc[:],
                     start=True,
                     stop=True,
                 )
-            y = [y_ps[d // 2][:, d % 2, :].rearrange("p (n a) -> p a n", a=2) for d in range(D)]
-            top = sb("top%d0" % h, [P, 2, P], F32)
-            nc.scalar.activation(top[:], y[0], ACT.Identity, bias=neg_nb[:, 0:1])
-            for d in range(1, D):
-                last, top = top, sb("top%d%d" % (h, d), [P, 2, P], F32)
-                for part in [slice(0, 2)] if d < D - 1 else [slice(0, 1), slice(1, 2)]:
-                    nc.vector.scalar_tensor_tensor(top[:, part, :], y[d][:, part, :], neg_nb[:, d : d + 1], last[:, part, :], ALU.add, ALU.max)
-            far.append(top)
 
-        for h in range(2):
-            rr = sb("rr%d" % h, [P, 2, V], F32)
-            res = sb("res%d" % h, [P, 2, V], F32)
-            for a in range(2):
-                o_ps = bank("h%d" % (2 * h + a), "o_ps%d%d" % (h, a), [P, V])
-                nc.tensor.transpose(o_ps[:], far[h][:, a, :], ident[:])
-                if h == 0:
-                    nc.scalar.activation(rr[:, a, :], o_ps[:], ACT.Relu, bias=own_t[:, h, a : a + 1], scale=-1.0)
+        top = {}
+        for i, (g0, n) in enumerate(pieces):
+            top[i, 0] = sb("top%d0" % i, [P, n * P], F32)
+            nc.scalar.activation(top[i, 0][:], y[i, 0], ACT.Identity, bias=neg_nb[:, 0:1])
+        for i, d in [(0, 1), (1, 1), (0, 2), (2, 1), (0, 3), (1, 2), (2, 2), (1, 3), (2, 3)]:
+            top[i, d] = sb("top%d%d" % (i, d), [P, pieces[i][1] * P], F32)
+            nc.vector.scalar_tensor_tensor(top[i, d][:], y[i, d], neg_nb[:, d : d + 1], top[i, d - 1][:], ALU.add, ALU.max)
+
+        for i, (g0, n) in enumerate(pieces):
+            rr = sb("rr%d" % i, [P, n, V], F32)
+            res = sb("res%d" % i, [P, n, V], F32)
+            last = i == len(pieces) - 1
+            for a in range(n):
+                g = g0 + a
+                o_ps = bank([4, 5, 0, 2][g], "o_ps%d" % g, [P, V])
+                nc.tensor.transpose(o_ps[:], top[i, D - 1][:, a * P : (a + 1) * P], ident[:])
+                if last:
+                    nc.vector.tensor_scalar(rr[:, a, :], o_ps[:], own_t[:, g : g + 1], 0.0, ALU.subtract, ALU.min)
                 else:
-                    nc.vector.tensor_scalar(rr[:, a, :], o_ps[:], own_t[:, h, a : a + 1], 0.0, ALU.subtract, ALU.min)
-            nc.scalar.activation(res[:], rr[:], ACT.Sqrt, bias=0.01, scale=1.0 if h == 0 else -1.0)
-            nc.sync.dma_start(out[h * HALF : (h + 1) * HALF, :].rearrange("(p a) v -> p a v", a=2), res[:])
+                    nc.scalar.activation(rr[:, a, :], o_ps[:], ACT.Relu, bias=own_t[:, g : g + 1], scale=-1.0)
+            nc.scalar.activation(res[:], rr[:], ACT.Sqrt, bias=eps[:], scale=-1.0 if last else 1.0)
+            nc.sync.dma_start(out[g0 * P : (g0 + n) * P, :].rearrange("(a p) v -> p a v", a=n), res[:])

@@ -21,7 +21,7 @@ ACT = mybir.ActivationFunctionType
 E_PLANE = 4
 NB_ROW = P - 1
 HALF = S // 2
-M_SCALAR = 96
+M_SCALAR = 72
 NB_VECTOR = 3 * W // 4
 
 
@@ -79,8 +79,8 @@ def tile_picked_ycham_root_p_kernel(tc, x_words, x_scales, w1, e_words, e_scales
         nc.vector.tensor_copy(nb_g[:], nb_t[:].indirect(oth_t[:]))
 
         w_bf = sb("w_bf", [P, 4 * H], BF16)
-        w_dst = w_bf[:].rearrange("p (t m j) -> p m t j", t=4, j=4)
-        w_src = w_raw[:].rearrange("p j (m t) -> p m t j", t=4)
+        w_dst = w_bf[:].rearrange("p (t m j) -> p m j t", t=4, j=4)
+        w_src = w_raw[:].rearrange("p j (m t) -> p m j t", t=4)
         nc.scalar.copy(w_dst[:, 0:M_SCALAR], w_src[:, 0:M_SCALAR])
         nc.vector.tensor_copy(w_dst[:, M_SCALAR:P], w_src[:, M_SCALAR:P])
 

@@ -62,12 +62,12 @@ def tile_picked_ycham_root_p_kernel(tc, x_words, x_scales, w1, e_words, e_scales
         nc.sync.dma_start(oth_t[:], oth)
         nc.sync.dma_start(nb_t[NB_ROW : NB_ROW + 1, :], nb[0:1, :])
         nc.sync.dma_start(w_raw[:, 0:1, :], w_rows[:, 0:1, :])
-        for q in range(4):
-            nc.sync.dma_start(es[32 * q + E_PLANE : 32 * q + E_PLANE + 4, :].bitcast(I32), e_scales[0, 4 * q : 4 * q + 4, :].bitcast(I32))
+        for r in range(4):
+            nc.sync.dma_start(es[E_PLANE + r : P : 32, :].bitcast(I32), e_scales[0, r:16:4, :].bitcast(I32))
         nc.sync.dma_start(w_raw[:, 1:4, :], w_rows[:, 1:4, :])
         nc.sync.dma_start(offs_t[:], offs)
-        for q in range(4):
-            nc.sync.dma_start(xs[32 * q : 32 * q + 4, :].bitcast(I32), x_scales[0, 4 * q : 4 * q + 4, :].bitcast(I32))
+        for r in range(4):
+            nc.sync.dma_start(xs[r:P:32, :].bitcast(I32), x_scales[0, r:16:4, :].bitcast(I32))
         nc.sync.dma_start(xw[:], x_words[0].rearrange("p n t -> p (n t)").bitcast(I32))
         nc.sync.dma_start(ew[:], e_words[0].rearrange("p n t -> p (n t)").bitcast(I32))
         with nc.allow_non_contiguous_dma(reason="512 norms, two to a partition and half"):

@@ -21,18 +21,22 @@ ACT = mybir.ActivationFunctionType
 E_PLANE = 4
 NB_ROW = P - 1
 HALF = S // 2
-M_SCALAR = 72
-NB_VECTOR = 3 * W // 4
+M_SCALAR = 96
+NB_VECTOR = W // 2
 
 
 def tile_picked_ycham_root_p_kernel(tc, x_words, x_scales, w1, e_words, e_scales, nb, own, offs, oth, out):
     nc = tc.nc
     with ExitStack() as ctx:
         keep = ctx.enter_context(tc.tile_pool(name="keep", bufs=1))
+        placed = ctx.enter_context(tc.tile_pool(name="placed", bufs=1))
         psum = ctx.enter_context(tc.psum_pool(name="psum", bufs=1))
 
         def sb(name, shape, dtype, tag=None):
             return keep.tile(shape, dtype, name=name, tag=tag or name, align_bytes=64)
+
+        def at(name, shape, dtype, offset):
+            return placed.tile(shape, dtype, name=name, tag=name, align_bytes=64, offset=offset)
 
         def bank(b, name, shape):
             return psum.tile(shape, F32, name=name, tag="bank%d" % b)
@@ -47,21 +51,21 @@ def tile_picked_ycham_root_p_kernel(tc, x_words, x_scales, w1, e_words, e_scales
         one = sb("one", [P, 1], F32)
         xs = sb("xs", [P, T], U8)
         xw = sb("xw", [P, T], I32)
-        ew = sb("ew", [P, W], I32)
+        ew = at("ew", [P, W], I32, 0)
 
         nc.vector.memset(es[:].bitcast(I32), 0)
-        nc.vector.memset(xs[:].bitcast(I32), 0)
+        nc.gpsimd.memset(xs[:].bitcast(I32), 0)
         nc.vector.memset(one[:], 1.0)
         nc.vector.memset(nb_t[0:NB_ROW, 0:NB_VECTOR], 0.0)
+        nc.gpsimd.memset(nb_t[0:NB_ROW, NB_VECTOR:W], 0.0)
         nc.scalar.activation(eps[:], one[:], ACT.Sqrt, scale=1e-4)
-        nc.scalar.activation(nb_t[0:NB_ROW, NB_VECTOR:W], eps[0:NB_ROW, :].to_broadcast([NB_ROW, W - NB_VECTOR]), ACT.Copy, scale=0.0)
         ident = sb("ident", [P, P], F32, tag="one")
         make_identity(nc, ident[:])
         w_rows = w1.rearrange("(p j) c -> p j c", j=4)
 
+        nc.sync.dma_start(w_raw[:, 0:1, :], w_rows[:, 0:1, :])
         nc.sync.dma_start(oth_t[:], oth)
         nc.sync.dma_start(nb_t[NB_ROW : NB_ROW + 1, :], nb[0:1, :])
-        nc.sync.dma_start(w_raw[:, 0:1, :], w_rows[:, 0:1, :])
         for r in range(4):
             nc.sync.dma_start(es[E_PLANE + r : P : 32, :].bitcast(I32), e_scales[0, r:16:4, :].bitcast(I32))
         nc.sync.dma_start(w_raw[:, 1:4, :], w_rows[:, 1:4, :])
@@ -105,8 +109,8 @@ def tile_picked_ycham_root_p_kernel(tc, x_words, x_scales, w1, e_words, e_scales
         ep_s = sb("ep_s", [P, U], U8, tag="xw")
         nc.vector.tensor_copy(ep_s[:].rearrange("p (d v) -> p d v", d=D), eg_s[:].rearrange("p (v d) -> p d v", d=D))
 
-        pieces = [(0, 2), (2, 1), (3, 1)]
-        piece_of = [0, 0, 1, 2]
+        pieces = [(0, 1), (1, 1), (2, 1), (3, 1)]
+        piece_of = [0, 1, 2, 3]
         h_bf = [sb("h_bf%d" % i, [P, 4 * n * P], BF16) for i, (g0, n) in enumerate(pieces)]
         for g in range(4):
             cols = slice(g * P, (g + 1) * P)
@@ -129,15 +133,15 @@ def tile_picked_ycham_root_p_kernel(tc, x_words, x_scales, w1, e_words, e_scales
 
         y = {}
         for i, (g0, n) in enumerate(pieces):
-            h_codes = sb("h_codes%d" % i, [P, n * P], U32, tag="ew" if i == 0 else None)
+            h_codes = at("h_codes%d" % i, [P, n * P], U32, 4 * g0 * P)
             h_sc = sb("h_sc%d" % i, [P, n * P], U8)
             nc.vector.quantize_mx(out=h_codes[:].bitcast(FP8X4), scales=h_sc[:], in_=h_bf[i][:])
             if n == 2:
                 for d in range(D):
-                    y[i, d] = bank(4 + d, "y_ps%d%d" % (i, d), [P, n * P])[:]
+                    y[i, d] = bank([6, 7, 0, 1][d], "y_ps%d%d" % (i, d), [P, n * P])[:]
             else:
-                y[i, 0] = bank(2 * i - 2, "y_first%d" % i, [P, P])[:]
-                rest = bank(2 * i - 1, "y_rest%d" % i, [P, D - 1, P])
+                y[i, 0] = bank((4 + 2 * i) % 8, "y_first%d" % i, [P, P])[:]
+                rest = bank((5 + 2 * i) % 8, "y_rest%d" % i, [P, D - 1, P])
                 for d in range(1, D):
                     y[i, d] = rest[:, d - 1, :]
             for d in range(D):
@@ -155,21 +159,22 @@ def tile_picked_ycham_root_p_kernel(tc, x_words, x_scales, w1, e_words, e_scales
         for i, (g0, n) in enumerate(pieces):
             top[i, 0] = sb("top%d0" % i, [P, n * P], F32)
             nc.scalar.activation(top[i, 0][:], y[i, 0], ACT.Identity, bias=neg_nb[:, 0:1])
-        for i, d in [(0, 1), (1, 1), (0, 2), (2, 1), (0, 3), (1, 2), (2, 2), (1, 3), (2, 3)]:
-            top[i, d] = sb("top%d%d" % (i, d), [P, pieces[i][1] * P], F32)
-            nc.vector.scalar_tensor_tensor(top[i, d][:], y[i, d], neg_nb[:, d : d + 1], top[i, d - 1][:], ALU.add, ALU.max)
+        for i, d in [(0, 1), (1, 1), (0, 2), (2, 1), (1, 2), (0, 3), (3, 1), (2, 2), (1, 3), (3, 2), (2, 3), (3, 3)]:
+            n = pieces[i][1]
+            top[i, d] = sb("top%d%d" % (i, d), [P, n * P], F32)
+            for part in [slice(0, n * P)] if d < D - 1 else [slice(a * P, (a + 1) * P) for a in range(n)]:
+                nc.vector.scalar_tensor_tensor(top[i, d][:, part], y[i, d][:, part], neg_nb[:, d : d + 1], top[i, d - 1][:, part], ALU.add, ALU.max)
 
-        for i, (g0, n) in enumerate(pieces):
-            rr = sb("rr%d" % i, [P, n, V], F32)
-            res = sb("res%d" % i, [P, n, V], F32)
-            last = i == len(pieces) - 1
-            for a in range(n):
-                g = g0 + a
-                o_ps = bank([4, 5, 0, 2][g], "o_ps%d" % g, [P, V])
-                nc.tensor.transpose(o_ps[:], top[i, D - 1][:, a * P : (a + 1) * P], ident[:])
-                if last:
-                    nc.vector.tensor_scalar(rr[:, a, :], o_ps[:], own_t[:, g : g + 1], 0.0, ALU.subtract, ALU.min)
-                else:
-                    nc.scalar.activation(rr[:, a, :], o_ps[:], ACT.Relu, bias=own_t[:, g : g + 1], scale=-1.0)
-            nc.scalar.activation(res[:], rr[:], ACT.Sqrt, bias=eps[:], scale=-1.0 if last else 1.0)
-            nc.sync.dma_start(out[g0 * P : (g0 + n) * P, :].rearrange("(a p) v -> p a v", a=n), res[:])
+        for g in range(4):
+            i = piece_of[g]
+            a = g - pieces[i][0]
+            rr = sb("rr%d" % g, [P, V], F32)
+            res = sb("res%d" % g, [P, V], F32)
+            o_ps = bank((4 + 2 * g) % 8, "o_ps%d" % g, [P, V])
+            nc.tensor.transpose(o_ps[:], top[i, D - 1][:, a * P : (a + 1) * P], ident[:])
+            if g < 2:
+                nc.scalar.activation(rr[:], o_ps[:], ACT.Relu, bias=own_t[:, g : g + 1], scale=-1.0)
+            else:
+                nc.vector.tensor_scalar(rr[:], o_ps[:], own_t[:, g : g + 1], 0.0, ALU.subtract, ALU.min)
+            nc.scalar.activation(res[:], rr[:], ACT.Sqrt, bias=eps[:], scale=1.0 if g < 2 else -1.0)
+            nc.sync.dma_start(out[g * P : (g + 1) * P, :], res[:])

@@ -22,7 +22,7 @@ E_PLANE = 4
 NB_ROW = P - 1
 HALF = S // 2
 M_SCALAR = 96
-NB_VECTOR = W // 2
+NB_VECTOR = 3 * W // 4
 
 
 def tile_picked_ycham_root_p_kernel(tc, x_words, x_scales, w1, e_words, e_scales, nb, own, offs, oth, out):
@@ -54,18 +54,18 @@ def tile_picked_ycham_root_p_kernel(tc, x_words, x_scales, w1, e_words, e_scales
         ew = at("ew", [P, W], I32, 0)
 
         nc.vector.memset(es[:].bitcast(I32), 0)
-        nc.gpsimd.memset(xs[:].bitcast(I32), 0)
+        nc.vector.memset(xs[:].bitcast(I32), 0)
         nc.vector.memset(one[:], 1.0)
         nc.vector.memset(nb_t[0:NB_ROW, 0:NB_VECTOR], 0.0)
-        nc.gpsimd.memset(nb_t[0:NB_ROW, NB_VECTOR:W], 0.0)
         nc.scalar.activation(eps[:], one[:], ACT.Sqrt, scale=1e-4)
+        nc.scalar.activation(nb_t[0:NB_ROW, NB_VECTOR:W], eps[0:NB_ROW, :].to_broadcast([NB_ROW, W - NB_VECTOR]), ACT.Copy, scale=0.0)
         ident = sb("ident", [P, P], F32, tag="one")
         make_identity(nc, ident[:])
         w_rows = w1.rearrange("(p j) c -> p j c", j=4)
 
-        nc.sync.dma_start(w_raw[:, 0:1, :], w_rows[:, 0:1, :])
         nc.sync.dma_start(oth_t[:], oth)
         nc.sync.dma_start(nb_t[NB_ROW : NB_ROW + 1, :], nb[0:1, :])
+        nc.sync.dma_start(w_raw[:, 0:1, :], w_rows[:, 0:1, :])
         for r in range(4):
             nc.sync.dma_start(es[E_PLANE + r : P : 32, :].bitcast(I32), e_scales[0, r:16:4, :].bitcast(I32))
         nc.sync.dma_start(w_raw[:, 1:4, :], w_rows[:, 1:4, :])

@@ -22,7 +22,6 @@ E_PLANE = 4
 NB_ROW = P - 1
 HALF = S // 2
 M_SCALAR = 96
-NB_VECTOR = 3 * W // 4
 
 
 def tile_picked_ycham_root_p_kernel(tc, x_words, x_scales, w1, e_words, e_scales, nb, own, offs, oth, out):
@@ -49,6 +48,7 @@ def tile_picked_ycham_root_p_kernel(tc, x_words, x_scales, w1, e_words, e_scales
         eps = sb("eps", [P, 1], F32)
         own_t = sb("own_t", [P, 4], F32)
         one = sb("one", [P, 1], F32)
+        ident = sb("ident", [P, P], F32)
         xs = sb("xs", [P, T], U8)
         xw = sb("xw", [P, T], I32)
         ew = at("ew", [P, W], I32, 0)
@@ -56,11 +56,10 @@ def tile_picked_ycham_root_p_kernel(tc, x_words, x_scales, w1, e_words, e_scales
         nc.vector.memset(es[:].bitcast(I32), 0)
         nc.vector.memset(xs[:].bitcast(I32), 0)
         nc.vector.memset(one[:], 1.0)
-        nc.vector.memset(nb_t[0:NB_ROW, 0:NB_VECTOR], 0.0)
+        nc.vector.memset(ident[:], 0.0)
+        nc.vector.memset(nb_t[0:NB_ROW, :].bitcast(I32), 0)
+        make_identity(nc, ident[:], nomemset=True)
         nc.scalar.activation(eps[:], one[:], ACT.Sqrt, scale=1e-4)
-        nc.scalar.activation(nb_t[0:NB_ROW, NB_VECTOR:W], eps[0:NB_ROW, :].to_broadcast([NB_ROW, W - NB_VECTOR]), ACT.Copy, scale=0.0)
-        ident = sb("ident", [P, P], F32, tag="one")
-        make_identity(nc, ident[:])
         w_rows = w1.rearrange("(p j) c -> p j c", j=4)
 
         nc.sync.dma_start(oth_t[:], oth)

@@ -18,10 +18,11 @@ FP8X4 = mybir.dt.float8_e4m3fn_x4
 ALU = mybir.AluOpType
 ACT = mybir.ActivationFunctionType
 
-E_PLANE = 4
+X_FIRST = 48
+E_FIRST = 112
+ROWS = 16
 NB_ROW = P - 1
 HALF = S // 2
-M_SCALAR = 96
 
 
 def tile_picked_ycham_root_p_kernel(tc, x_words, x_scales, w1, e_words, e_scales, nb, own, offs, oth, out):
@@ -44,60 +45,68 @@ def tile_picked_ycham_root_p_kernel(tc, x_words, x_scales, w1, e_words, e_scales
         oth_t = sb("oth_t", [P, U // 16], U16)
         es = sb("es", [P, W], U8)
         nb_t = sb("nb_t", [P, W], F32)
-        w_raw = sb("w_raw", [P, 4, H], F32)
+        w_raw = [sb("w_raw%d" % a, [P, 4, H // 2], F32) for a in range(2)]
         eps = sb("eps", [P, 1], F32)
-        own_t = sb("own_t", [P, 4], F32)
         one = sb("one", [P, 1], F32)
         ident = sb("ident", [P, P], F32)
-        xs = sb("xs", [P, T], U8)
+        xs = at("xs", [P, T], U8, 0)
+        x_plane = sb("x_plane", [P, S], U8)
+        e_plane = sb("e_plane", [P, U], U8)
         xw = sb("xw", [P, T], I32)
-        ew = at("ew", [P, W], I32, 0)
 
-        nc.vector.memset(es[:].bitcast(I32), 0)
-        nc.vector.memset(xs[:].bitcast(I32), 0)
         nc.vector.memset(one[:], 1.0)
+        nc.vector.memset(xs[0:X_FIRST, :].bitcast(I32), 0)
+        nc.vector.memset(xs[X_FIRST + ROWS : P, :].bitcast(I32), 0)
+        nc.vector.memset(es[0:E_FIRST, :].bitcast(I32), 0)
         nc.vector.memset(ident[:], 0.0)
-        nc.vector.memset(nb_t[0:NB_ROW, :].bitcast(I32), 0)
+        nc.vector.memset(x_plane[:].bitcast(I32), 0)
+        nc.vector.memset(e_plane[:].bitcast(I32), 0)
         make_identity(nc, ident[:], nomemset=True)
         nc.scalar.activation(eps[:], one[:], ACT.Sqrt, scale=1e-4)
+        nc.scalar.activation(nb_t[0:NB_ROW, :], eps[0:NB_ROW, :].to_broadcast([NB_ROW, W]), ACT.Copy, scale=0.0)
         w_rows = w1.rearrange("(p j) c -> p j c", j=4)
 
-        nc.sync.dma_start(oth_t[:], oth)
-        nc.sync.dma_start(nb_t[NB_ROW : NB_ROW + 1, :], nb[0:1, :])
-        nc.sync.dma_start(w_raw[:, 0:1, :], w_rows[:, 0:1, :])
-        for r in range(4):
-            nc.sync.dma_start(es[E_PLANE + r : P : 32, :].bitcast(I32), e_scales[0, r:16:4, :].bitcast(I32))
-        nc.sync.dma_start(w_raw[:, 1:4, :], w_rows[:, 1:4, :])
         nc.sync.dma_start(offs_t[:], offs)
-        for r in range(4):
-            nc.sync.dma_start(xs[r:P:32, :].bitcast(I32), x_scales[0, r:16:4, :].bitcast(I32))
+        nc.sync.dma_start(xs[X_FIRST : X_FIRST + ROWS, :].bitcast(I32), x_scales[0].bitcast(I32))
+        nc.sync.dma_start(w_raw[0][:], w_rows[:, :, 0 : H // 2])
+        nc.sync.dma_start(oth_t[:], oth)
+        nc.sync.dma_start(es[E_FIRST : E_FIRST + ROWS, :].bitcast(I32), e_scales[0].bitcast(I32))
+        nc.sync.dma_start(nb_t[NB_ROW : NB_ROW + 1, :], nb[0:1, :])
+        nc.sync.dma_start(w_raw[1][:], w_rows[:, :, H // 2 : H])
         nc.sync.dma_start(xw[:], x_words[0].rearrange("p n t -> p (n t)").bitcast(I32))
+
+        xg_s = sb("xg_s", [P, S], U8)
+        nc.vector.tensor_copy(xg_s[:], xs[:].indirect(offs_t[:]))
+        for r in range(4):
+            nc.sync.dma_start(x_plane[r:P:32, :].bitcast(I32), xg_s[X_FIRST + r : X_FIRST + ROWS : 4, :].bitcast(I32))
+        ew = at("ew", [P, W], I32, 0)
         nc.sync.dma_start(ew[:], e_words[0].rearrange("p n t -> p (n t)").bitcast(I32))
-        with nc.allow_non_contiguous_dma(reason="512 norms, two to a partition and half"):
-            nc.sync.dma_start(own_t[:], own.rearrange("(g p) o -> p (g o)", g=4))
 
         eg_s = sb("eg_s", [P, U], U8)
         nc.vector.tensor_copy(eg_s[:], es[:].indirect(oth_t[:]))
         nb_g = sb("nb_g", [P, U], F32)
         nc.vector.tensor_copy(nb_g[:], nb_t[:].indirect(oth_t[:]))
+        ep_s = sb("ep_s", [P, U], U8)
+        nc.vector.tensor_copy(ep_s[:].rearrange("p (d v) -> p d v", d=D), eg_s[:].rearrange("p (v d) -> p d v", d=D))
+        for r in range(4):
+            nc.sync.dma_start(e_plane[r:P:32, :].bitcast(I32), ep_s[E_FIRST + r : E_FIRST + ROWS : 4, :].bitcast(I32))
+        own_t = sb("own_t", [P, 4], F32, tag="eg_s")
+        with nc.allow_non_contiguous_dma(reason="512 norms, four to a partition"):
+            nc.sync.dma_start(own_t[:], own.rearrange("(g p) o -> p (g o)", g=4))
 
         w_bf = sb("w_bf", [P, 4 * H], BF16)
         w_dst = w_bf[:].rearrange("p (t m j) -> p m j t", t=4, j=4)
-        w_src = w_raw[:].rearrange("p j (m t) -> p m j t", t=4)
-        nc.scalar.copy(w_dst[:, 0:M_SCALAR], w_src[:, 0:M_SCALAR])
-        nc.vector.tensor_copy(w_dst[:, M_SCALAR:P], w_src[:, M_SCALAR:P])
+        for a in range(2):
+            nc.scalar.copy(w_dst[:, a * (P // 2) : (a + 1) * (P // 2)], w_raw[a][:].rearrange("p j (m t) -> p m j t", t=4))
 
-        xg_s = sb("xg_s", [P, S], U8)
-        nc.vector.tensor_copy(xg_s[:], xs[:].indirect(offs_t[:]))
-
-        w_codes = sb("w_codes", [P, H], U32, tag="xs")
+        w_codes = sb("w_codes", [P, H], U32)
         w_sc = sb("w_sc", [P, H], U8)
         nc.vector.quantize_mx(out=w_codes[:].bitcast(FP8X4), scales=w_sc[:], in_=w_bf[:])
 
         nb_ps = bank(7, "nb_ps", [P, D, P])
         for d in range(D):
             nc.tensor.transpose(nb_ps[:, d, :], nb_g[:, d : U : D], ident[:])
-        neg_nb = sb("neg_nb", [P, D], F32, tag="w_raw")
+        neg_nb = sb("neg_nb", [P, D], F32, tag="w_raw1")
         nc.scalar.activation(neg_nb[:], nb_ps[:, :, NB_ROW], ACT.Copy, scale=-1.0)
 
         xg_w = []
@@ -105,12 +114,9 @@ def tile_picked_ycham_root_p_kernel(tc, x_words, x_scales, w1, e_words, e_scales
             xg_w.append(sb("xg_w%d" % h, [P, HALF], U32))
             nc.vector.tensor_copy(xg_w[h][:], xw[:].bitcast(U32).indirect(offs_t[:, 16 * h : 16 * (h + 1)]))
 
-        ep_s = sb("ep_s", [P, U], U8, tag="xw")
-        nc.vector.tensor_copy(ep_s[:].rearrange("p (d v) -> p d v", d=D), eg_s[:].rearrange("p (v d) -> p d v", d=D))
-
         pieces = [(0, 1), (1, 1), (2, 1), (3, 1)]
         piece_of = [0, 1, 2, 3]
-        h_bf = [sb("h_bf%d" % i, [P, 4 * n * P], BF16) for i, (g0, n) in enumerate(pieces)]
+        h_bf = [at("h_bf%d" % i, [P, 4 * n * P], BF16, 4 * W + 8 * P * (i + 1)) for i, (g0, n) in enumerate(pieces)]
         for g in range(4):
             cols = slice(g * P, (g + 1) * P)
             h_ps = bank(g, "h_ps%d" % g, [P, 4, P])
@@ -120,7 +126,7 @@ def tile_picked_ycham_root_p_kernel(tc, x_words, x_scales, w1, e_words, e_scales
                     lhsT=w_codes[:, t * P : (t + 1) * P].bitcast(FP8X4),
                     lhsT_scale=w_sc[:, t * P : (t + 1) * P],
                     rhs=xg_w[g // 2][:, (g % 2) * P : (g % 2 + 1) * P].bitcast(FP8X4),
-                    rhs_scale=xg_s[:, cols],
+                    rhs_scale=x_plane[:, cols],
                     start=True,
                     stop=True,
                 )
@@ -147,7 +153,7 @@ def tile_picked_ycham_root_p_kernel(tc, x_words, x_scales, w1, e_words, e_scales
                 nc.tensor.matmul_mx(
                     out=y[i, d],
                     lhsT=ep_w[:, d * V : (d + 1) * V].bitcast(FP8X4),
-                    lhsT_scale=ep_s[E_PLANE:P, d * V : (d + 1) * V],
+                    lhsT_scale=e_plane[:, d * V : (d + 1) * V],
                     rhs=h_codes[:].bitcast(FP8X4),
                     rhs_scale=h_sc[:],
                     start=True,

@@ -45,7 +45,7 @@ def tile_picked_ycham_root_p_kernel(tc, x_words, x_scales, w1, e_words, e_scales
         oth_t = sb("oth_t", [P, U // 16], U16)
         es = sb("es", [P, W], U8)
         nb_t = sb("nb_t", [P, W], F32)
-        w_raw = [sb("w_raw%d" % a, [P, 4, H // 2], F32) for a in range(2)]
+        w_raw = sb("w_raw", [P, 4, H], F32)
         eps = sb("eps", [P, 1], F32)
         one = sb("one", [P, 1], F32)
         ident = sb("ident", [P, P], F32)
@@ -54,6 +54,7 @@ def tile_picked_ycham_root_p_kernel(tc, x_words, x_scales, w1, e_words, e_scales
         e_plane = sb("e_plane", [P, U], U8)
         xw = sb("xw", [P, T], I32)
 
+        nc.scalar.dma_start(xs[X_FIRST : X_FIRST + ROWS, :].bitcast(I32), x_scales[0].bitcast(I32))
         nc.vector.memset(one[:], 1.0)
         nc.vector.memset(xs[0:X_FIRST, :].bitcast(I32), 0)
         nc.vector.memset(xs[X_FIRST + ROWS : P, :].bitcast(I32), 0)
@@ -67,12 +68,11 @@ def tile_picked_ycham_root_p_kernel(tc, x_words, x_scales, w1, e_words, e_scales
         w_rows = w1.rearrange("(p j) c -> p j c", j=4)
 
         nc.sync.dma_start(offs_t[:], offs)
-        nc.sync.dma_start(xs[X_FIRST : X_FIRST + ROWS, :].bitcast(I32), x_scales[0].bitcast(I32))
-        nc.sync.dma_start(w_raw[0][:], w_rows[:, :, 0 : H // 2])
+        nc.sync.dma_start(w_raw[:, 0:1, :], w_rows[:, 0:1, :])
         nc.sync.dma_start(oth_t[:], oth)
         nc.sync.dma_start(es[E_FIRST : E_FIRST + ROWS, :].bitcast(I32), e_scales[0].bitcast(I32))
         nc.sync.dma_start(nb_t[NB_ROW : NB_ROW + 1, :], nb[0:1, :])
-        nc.sync.dma_start(w_raw[1][:], w_rows[:, :, H // 2 : H])
+        nc.sync.dma_start(w_raw[:, 1:4, :], w_rows[:, 1:4, :])
         nc.sync.dma_start(xw[:], x_words[0].rearrange("p n t -> p (n t)").bitcast(I32))
 
         xg_s = sb("xg_s", [P, S], U8)
@@ -84,8 +84,6 @@ def tile_picked_ycham_root_p_kernel(tc, x_words, x_scales, w1, e_words, e_scales
 
         eg_s = sb("eg_s", [P, U], U8)
         nc.vector.tensor_copy(eg_s[:], es[:].indirect(oth_t[:]))
-        nb_g = sb("nb_g", [P, U], F32)
-        nc.vector.tensor_copy(nb_g[:], nb_t[:].indirect(oth_t[:]))
         ep_s = sb("ep_s", [P, U], U8)
         nc.vector.tensor_copy(ep_s[:].rearrange("p (d v) -> p d v", d=D), eg_s[:].rearrange("p (v d) -> p d v", d=D))
         for r in range(4):
@@ -95,24 +93,27 @@ def tile_picked_ycham_root_p_kernel(tc, x_words, x_scales, w1, e_words, e_scales
             nc.sync.dma_start(own_t[:], own.rearrange("(g p) o -> p (g o)", g=4))
 
         w_bf = sb("w_bf", [P, 4 * H], BF16)
-        w_dst = w_bf[:].rearrange("p (t m j) -> p m j t", t=4, j=4)
-        for a in range(2):
-            nc.scalar.copy(w_dst[:, a * (P // 2) : (a + 1) * (P // 2)], w_raw[a][:].rearrange("p j (m t) -> p m j t", t=4))
+        w_dst = w_bf[:].rearrange("p (t m j) -> p m t j", t=4, j=4)
+        w_src = w_raw[:].rearrange("p j (m t) -> p m t j", t=4)
+        nc.scalar.copy(w_dst, w_src)
 
-        w_codes = sb("w_codes", [P, H], U32)
-        w_sc = sb("w_sc", [P, H], U8)
-        nc.vector.quantize_mx(out=w_codes[:].bitcast(FP8X4), scales=w_sc[:], in_=w_bf[:])
+        nb_g = sb("nb_g", [P, U], F32)
+        nc.vector.tensor_copy(nb_g[:], nb_t[:].indirect(oth_t[:]))
 
         nb_ps = bank(7, "nb_ps", [P, D, P])
         for d in range(D):
             nc.tensor.transpose(nb_ps[:, d, :], nb_g[:, d : U : D], ident[:])
-        neg_nb = sb("neg_nb", [P, D], F32, tag="w_raw1")
+        neg_nb = sb("neg_nb", [P, D], F32, tag="w_raw")
         nc.scalar.activation(neg_nb[:], nb_ps[:, :, NB_ROW], ACT.Copy, scale=-1.0)
 
-        xg_w = []
-        for h in range(2):
-            xg_w.append(sb("xg_w%d" % h, [P, HALF], U32))
-            nc.vector.tensor_copy(xg_w[h][:], xw[:].bitcast(U32).indirect(offs_t[:, 16 * h : 16 * (h + 1)]))
+        xg_w = [sb("xg_w0", [P, HALF], U32)]
+        nc.vector.tensor_copy(xg_w[0][:], xw[:].bitcast(U32).indirect(offs_t[:, 0:16]))
+        w_codes = sb("w_codes", [P, H], U32, tag="xg_s")
+        w_sc = sb("w_sc", [P, H], U8)
+        for t in range(4):
+            nc.vector.quantize_mx(out=w_codes[:, t * P : (t + 1) * P].bitcast(FP8X4), scales=w_sc[:, t * P : (t + 1) * P], in_=w_bf[:, 4 * t * P : 4 * (t + 1) * P])
+        xg_w.append(sb("xg_w1", [P, HALF], U32, tag="w_bf"))
+        nc.vector.tensor_copy(xg_w[1][:], xw[:].bitcast(U32).indirect(offs_t[:, 16:32]))
 
         pieces = [(0, 1), (1, 1), (2, 1), (3, 1)]
         piece_of = [0, 1, 2, 3]
@@ -182,4 +183,4 @@ def tile_picked_ycham_root_p_kernel(tc, x_words, x_scales, w1, e_words, e_scales
             else:
                 nc.vector.tensor_scalar(rr[:], o_ps[:], own_t[:, g : g + 1], 0.0, ALU.subtract, ALU.min)
             nc.scalar.activation(res[:], rr[:], ACT.Sqrt, bias=eps[:], scale=1.0 if g < 2 else -1.0)
-            nc.sync.dma_start(out[g * P : (g + 1) * P, :], res[:])
+            (nc.scalar if g == 3 else nc.sync).dma_start(out[g * P : (g + 1) * P, :], res[:])

@@ -23,6 +23,9 @@ E_FIRST = 112
 ROWS = 16
 NB_ROW = P - 1
 HALF = S // 2
+T_ORDER = (3, 0, 1, 2)
+X_HOLD = 16384
+E_HOLD = 24576
 
 
 def tile_picked_ycham_root_p_kernel(tc, x_words, x_scales, w1, e_words, e_scales, nb, own, offs, oth, out):
@@ -56,10 +59,10 @@ def tile_picked_ycham_root_p_kernel(tc, x_words, x_scales, w1, e_words, e_scales
 
         nc.scalar.dma_start(xs[X_FIRST : X_FIRST + ROWS, :].bitcast(I32), x_scales[0].bitcast(I32))
         nc.vector.memset(one[:], 1.0)
+        nc.vector.memset(ident[:], 0.0)
         nc.vector.memset(xs[0:X_FIRST, :].bitcast(I32), 0)
         nc.vector.memset(xs[X_FIRST + ROWS : P, :].bitcast(I32), 0)
         nc.vector.memset(es[0:E_FIRST, :].bitcast(I32), 0)
-        nc.vector.memset(ident[:], 0.0)
         nc.vector.memset(x_plane[:].bitcast(I32), 0)
         nc.vector.memset(e_plane[:].bitcast(I32), 0)
         make_identity(nc, ident[:], nomemset=True)
@@ -75,7 +78,7 @@ def tile_picked_ycham_root_p_kernel(tc, x_words, x_scales, w1, e_words, e_scales
         nc.sync.dma_start(w_raw[:, 1:4, :], w_rows[:, 1:4, :])
         nc.sync.dma_start(xw[:], x_words[0].rearrange("p n t -> p (n t)").bitcast(I32))
 
-        xg_s = sb("xg_s", [P, S], U8)
+        xg_s = at("xg_s", [P, S], U8, X_HOLD + 4 * H - S // 2)
         nc.vector.tensor_copy(xg_s[:], xs[:].indirect(offs_t[:]))
         for r in range(4):
             nc.sync.dma_start(x_plane[r:P:32, :].bitcast(I32), xg_s[X_FIRST + r : X_FIRST + ROWS : 4, :].bitcast(I32))
@@ -84,7 +87,7 @@ def tile_picked_ycham_root_p_kernel(tc, x_words, x_scales, w1, e_words, e_scales
 
         eg_s = sb("eg_s", [P, U], U8)
         nc.vector.tensor_copy(eg_s[:], es[:].indirect(oth_t[:]))
-        ep_s = sb("ep_s", [P, U], U8)
+        ep_s = at("ep_s", [P, U], U8, E_HOLD)
         nc.vector.tensor_copy(ep_s[:].rearrange("p (d v) -> p d v", d=D), eg_s[:].rearrange("p (v d) -> p d v", d=D))
         for r in range(4):
             nc.sync.dma_start(e_plane[r:P:32, :].bitcast(I32), ep_s[E_FIRST + r : E_FIRST + ROWS : 4, :].bitcast(I32))
@@ -92,11 +95,14 @@ def tile_picked_ycham_root_p_kernel(tc, x_words, x_scales, w1, e_words, e_scales
         with nc.allow_non_contiguous_dma(reason="512 norms, four to a partition"):
             nc.sync.dma_start(own_t[:], own.rearrange("(g p) o -> p (g o)", g=4))
 
-        w_bf = sb("w_bf", [P, 4 * H], BF16)
-        w_dst = w_bf[:].rearrange("p (t m j) -> p m t j", t=4, j=4)
-        w_src = w_raw[:].rearrange("p j (m t) -> p m t j", t=4)
-        nc.scalar.copy(w_dst, w_src)
-
+        w_src = w_raw[:].rearrange("p j (m t) -> p t m j", t=4)
+        w_pair = sb("w_pair", [P, 2, 4 * P], BF16)
+        w_third = sb("w_third", [P, 4 * P], BF16)
+        w_last = sb("w_last", [P, 4 * P], BF16)
+        nc.scalar.copy(w_pair[:].rearrange("p t (m j) -> p m t j", j=4), w_src[:, 0:2].rearrange("p t m j -> p m t j"))
+        nc.scalar.copy(w_third[:].rearrange("p (m j) -> p m j", j=4), w_src[:, 2])
+        nc.vector.tensor_copy(w_last[:].rearrange("p (m j) -> p m j", j=4), w_src[:, 3])
+        w_bf = [w_pair[:, 0, :], w_pair[:, 1, :], w_third[:], w_last[:]]
         nb_g = sb("nb_g", [P, U], F32)
         nc.vector.tensor_copy(nb_g[:], nb_t[:].indirect(oth_t[:]))
 
@@ -108,11 +114,11 @@ def tile_picked_ycham_root_p_kernel(tc, x_words, x_scales, w1, e_words, e_scales
 
         xg_w = [sb("xg_w0", [P, HALF], U32)]
         nc.vector.tensor_copy(xg_w[0][:], xw[:].bitcast(U32).indirect(offs_t[:, 0:16]))
-        w_codes = sb("w_codes", [P, H], U32, tag="xg_s")
+        w_codes = at("w_codes", [P, H], U32, X_HOLD)
         w_sc = sb("w_sc", [P, H], U8)
-        for t in range(4):
-            nc.vector.quantize_mx(out=w_codes[:, t * P : (t + 1) * P].bitcast(FP8X4), scales=w_sc[:, t * P : (t + 1) * P], in_=w_bf[:, 4 * t * P : 4 * (t + 1) * P])
-        xg_w.append(sb("xg_w1", [P, HALF], U32, tag="w_bf"))
+        for t in T_ORDER:
+            nc.vector.quantize_mx(out=w_codes[:, t * P : (t + 1) * P].bitcast(FP8X4), scales=w_sc[:, t * P : (t + 1) * P], in_=w_bf[t])
+        xg_w.append(at("xg_w1", [P, HALF], U32, X_HOLD + 4 * H))
         nc.vector.tensor_copy(xg_w[1][:], xw[:].bitcast(U32).indirect(offs_t[:, 16:32]))
 
         pieces = [(0, 1), (1, 1), (2, 1), (3, 1)]
@@ -121,7 +127,7 @@ def tile_picked_ycham_root_p_kernel(tc, x_words, x_scales, w1, e_words, e_scales
         for g in range(4):
             cols = slice(g * P, (g + 1) * P)
             h_ps = bank(g, "h_ps%d" % g, [P, 4, P])
-            for t in range(4):
+            for t in T_ORDER:
                 nc.tensor.matmul_mx(
                     out=h_ps[:, t, :],
                     lhsT=w_codes[:, t * P : (t + 1) * P].bitcast(FP8X4),
@@ -139,8 +145,8 @@ def tile_picked_ycham_root_p_kernel(tc, x_words, x_scales, w1, e_words, e_scales
 
         y = {}
         for i, (g0, n) in enumerate(pieces):
-            h_codes = at("h_codes%d" % i, [P, n * P], U32, 4 * g0 * P)
-            h_sc = sb("h_sc%d" % i, [P, n * P], U8)
+            h_codes = sb("h_codes%d" % i, [P, n * P], U32)
+            h_sc = at("h_sc%d" % i, [P, n * P], U8, E_HOLD + g0 * P)
             nc.vector.quantize_mx(out=h_codes[:].bitcast(FP8X4), scales=h_sc[:], in_=h_bf[i][:])
             if n == 2:
                 for d in range(D):

@@ -18,12 +18,15 @@ FP8X4 = mybir.dt.float8_e4m3fn_x4
 ALU = mybir.AluOpType
 ACT = mybir.ActivationFunctionType
 
-X_FIRST = 48
-E_FIRST = 112
-ROWS = 16
-NB_ROW = P - 1
+PACK = 4
+GROUPS = S // P
 HALF = S // 2
-T_ORDER = (3, 0, 1, 2)
+ROWS = 16
+X_FIRST = 112
+E_FIRST = 48
+NB_ROW = P - 1
+SCALAR_CLAMPS = 2
+H_AT = 4 * W + 8 * P
 X_HOLD = 16384
 E_HOLD = 24576
 
@@ -48,7 +51,7 @@ def tile_picked_ycham_root_p_kernel(tc, x_words, x_scales, w1, e_words, e_scales
         oth_t = sb("oth_t", [P, U // 16], U16)
         es = sb("es", [P, W], U8)
         nb_t = sb("nb_t", [P, W], F32)
-        w_raw = sb("w_raw", [P, 4, H], F32)
+        w_raw = sb("w_raw", [P, PACK, H], F32)
         eps = sb("eps", [P, 1], F32)
         one = sb("one", [P, 1], F32)
         ident = sb("ident", [P, P], F32)
@@ -58,24 +61,25 @@ def tile_picked_ycham_root_p_kernel(tc, x_words, x_scales, w1, e_words, e_scales
         xw = sb("xw", [P, T], I32)
 
         nc.scalar.dma_start(xs[X_FIRST : X_FIRST + ROWS, :].bitcast(I32), x_scales[0].bitcast(I32))
+
         nc.vector.memset(one[:], 1.0)
         nc.vector.memset(ident[:], 0.0)
         nc.vector.memset(xs[0:X_FIRST, :].bitcast(I32), 0)
-        nc.vector.memset(xs[X_FIRST + ROWS : P, :].bitcast(I32), 0)
         nc.vector.memset(es[0:E_FIRST, :].bitcast(I32), 0)
+        nc.vector.memset(es[E_FIRST + ROWS : P, :].bitcast(I32), 0)
         nc.vector.memset(x_plane[:].bitcast(I32), 0)
         nc.vector.memset(e_plane[:].bitcast(I32), 0)
         make_identity(nc, ident[:], nomemset=True)
         nc.scalar.activation(eps[:], one[:], ACT.Sqrt, scale=1e-4)
         nc.scalar.activation(nb_t[0:NB_ROW, :], eps[0:NB_ROW, :].to_broadcast([NB_ROW, W]), ACT.Copy, scale=0.0)
-        w_rows = w1.rearrange("(p j) c -> p j c", j=4)
+        w_rows = w1.rearrange("(p j) c -> p j c", j=PACK)
 
         nc.sync.dma_start(offs_t[:], offs)
         nc.sync.dma_start(w_raw[:, 0:1, :], w_rows[:, 0:1, :])
         nc.sync.dma_start(oth_t[:], oth)
         nc.sync.dma_start(es[E_FIRST : E_FIRST + ROWS, :].bitcast(I32), e_scales[0].bitcast(I32))
         nc.sync.dma_start(nb_t[NB_ROW : NB_ROW + 1, :], nb[0:1, :])
-        nc.sync.dma_start(w_raw[:, 1:4, :], w_rows[:, 1:4, :])
+        nc.sync.dma_start(w_raw[:, 1:PACK, :], w_rows[:, 1:PACK, :])
         nc.sync.dma_start(xw[:], x_words[0].rearrange("p n t -> p (n t)").bitcast(I32))
 
         xg_s = at("xg_s", [P, S], U8, X_HOLD + 4 * H - S // 2)
@@ -91,21 +95,19 @@ def tile_picked_ycham_root_p_kernel(tc, x_words, x_scales, w1, e_words, e_scales
         nc.vector.tensor_copy(ep_s[:].rearrange("p (d v) -> p d v", d=D), eg_s[:].rearrange("p (v d) -> p d v", d=D))
         for r in range(4):
             nc.sync.dma_start(e_plane[r:P:32, :].bitcast(I32), ep_s[E_FIRST + r : E_FIRST + ROWS : 4, :].bitcast(I32))
-        own_t = sb("own_t", [P, 4], F32, tag="eg_s")
-        with nc.allow_non_contiguous_dma(reason="512 norms, four to a partition"):
-            nc.sync.dma_start(own_t[:], own.rearrange("(g p) o -> p (g o)", g=4))
+        own_t = sb("own_t", [P, GROUPS], F32, tag="eg_s")
+        with nc.allow_non_contiguous_dma(reason="512 norms, one to a partition and group"):
+            nc.sync.dma_start(own_t[:], own.rearrange("(g p) o -> p (g o)", g=GROUPS))
 
-        w_src = w_raw[:].rearrange("p j (m t) -> p t m j", t=4)
-        w_pair = sb("w_pair", [P, 2, 4 * P], BF16)
-        w_third = sb("w_third", [P, 4 * P], BF16)
-        w_last = sb("w_last", [P, 4 * P], BF16)
-        nc.scalar.copy(w_pair[:].rearrange("p t (m j) -> p m t j", j=4), w_src[:, 0:2].rearrange("p t m j -> p m t j"))
-        nc.scalar.copy(w_third[:].rearrange("p (m j) -> p m j", j=4), w_src[:, 2])
-        nc.vector.tensor_copy(w_last[:].rearrange("p (m j) -> p m j", j=4), w_src[:, 3])
-        w_bf = [w_pair[:, 0, :], w_pair[:, 1, :], w_third[:], w_last[:]]
+        w_src = w_raw[:].rearrange("p j (m t) -> p t m j", t=PACK)
+        w_bf = []
+        for a in range(2):
+            w_pair = sb("w_pair%d" % a, [P, 2, PACK * P], BF16)
+            nc.scalar.copy(w_pair[:].rearrange("p t (m j) -> p m j t", j=PACK), w_src[:, 2 * a : 2 * a + 2].rearrange("p t m j -> p m j t"))
+            w_bf.extend([w_pair[:, 0, :], w_pair[:, 1, :]])
+
         nb_g = sb("nb_g", [P, U], F32)
         nc.vector.tensor_copy(nb_g[:], nb_t[:].indirect(oth_t[:]))
-
         nb_ps = bank(7, "nb_ps", [P, D, P])
         for d in range(D):
             nc.tensor.transpose(nb_ps[:, d, :], nb_g[:, d : U : D], ident[:])
@@ -113,52 +115,44 @@ def tile_picked_ycham_root_p_kernel(tc, x_words, x_scales, w1, e_words, e_scales
         nc.scalar.activation(neg_nb[:], nb_ps[:, :, NB_ROW], ACT.Copy, scale=-1.0)
 
         xg_w = [sb("xg_w0", [P, HALF], U32)]
-        nc.vector.tensor_copy(xg_w[0][:], xw[:].bitcast(U32).indirect(offs_t[:, 0:16]))
+        nc.vector.tensor_copy(xg_w[0][:], xw[:].bitcast(U32).indirect(offs_t[:, 0 : HALF // 16]))
         w_codes = at("w_codes", [P, H], U32, X_HOLD)
         w_sc = sb("w_sc", [P, H], U8)
-        for t in T_ORDER:
+        for t in range(PACK):
             nc.vector.quantize_mx(out=w_codes[:, t * P : (t + 1) * P].bitcast(FP8X4), scales=w_sc[:, t * P : (t + 1) * P], in_=w_bf[t])
         xg_w.append(at("xg_w1", [P, HALF], U32, X_HOLD + 4 * H))
-        nc.vector.tensor_copy(xg_w[1][:], xw[:].bitcast(U32).indirect(offs_t[:, 16:32]))
+        nc.vector.tensor_copy(xg_w[1][:], xw[:].bitcast(U32).indirect(offs_t[:, HALF // 16 : S // 16]))
 
-        pieces = [(0, 1), (1, 1), (2, 1), (3, 1)]
-        piece_of = [0, 1, 2, 3]
-        h_bf = [at("h_bf%d" % i, [P, 4 * n * P], BF16, 4 * W + 8 * P * (i + 1)) for i, (g0, n) in enumerate(pieces)]
-        for g in range(4):
-            cols = slice(g * P, (g + 1) * P)
-            h_ps = bank(g, "h_ps%d" % g, [P, 4, P])
-            for t in T_ORDER:
+        h_bf = [at("h_bf%d" % g, [P, PACK * P], BF16, H_AT + 2 * PACK * P * g) for g in range(GROUPS)]
+        for g in range(GROUPS):
+            h_ps = bank(g, "h_ps%d" % g, [P, PACK, P])
+            for t in range(PACK):
                 nc.tensor.matmul_mx(
                     out=h_ps[:, t, :],
                     lhsT=w_codes[:, t * P : (t + 1) * P].bitcast(FP8X4),
                     lhsT_scale=w_sc[:, t * P : (t + 1) * P],
                     rhs=xg_w[g // 2][:, (g % 2) * P : (g % 2 + 1) * P].bitcast(FP8X4),
-                    rhs_scale=x_plane[:, cols],
+                    rhs_scale=x_plane[:, g * P : (g + 1) * P],
                     start=True,
                     stop=True,
                 )
-            g_in = g - pieces[piece_of[g]][0]
-            nc.scalar.copy(h_bf[piece_of[g]][:, 4 * g_in * P : 4 * (g_in + 1) * P].rearrange("p (n t) -> p n t", t=4), h_ps[:].rearrange("p t n -> p n t"))
+            nc.scalar.copy(h_bf[g][:].rearrange("p (n t) -> p n t", t=PACK), h_ps[:].rearrange("p t n -> p n t"))
 
         ep_w = sb("ep_w", [P, U], U32)
         nc.vector.tensor_copy(ep_w[:].rearrange("p (d v) -> p v d", d=D), ew[:].bitcast(U32).indirect(oth_t[:]))
 
         y = {}
-        for i, (g0, n) in enumerate(pieces):
-            h_codes = sb("h_codes%d" % i, [P, n * P], U32)
-            h_sc = at("h_sc%d" % i, [P, n * P], U8, E_HOLD + g0 * P)
-            nc.vector.quantize_mx(out=h_codes[:].bitcast(FP8X4), scales=h_sc[:], in_=h_bf[i][:])
-            if n == 2:
-                for d in range(D):
-                    y[i, d] = bank([6, 7, 0, 1][d], "y_ps%d%d" % (i, d), [P, n * P])[:]
-            else:
-                y[i, 0] = bank((4 + 2 * i) % 8, "y_first%d" % i, [P, P])[:]
-                rest = bank((5 + 2 * i) % 8, "y_rest%d" % i, [P, D - 1, P])
-                for d in range(1, D):
-                    y[i, d] = rest[:, d - 1, :]
+        for g in range(GROUPS):
+            h_codes = sb("h_codes%d" % g, [P, P], U32)
+            h_sc = at("h_sc%d" % g, [P, P], U8, E_HOLD + g * P)
+            nc.vector.quantize_mx(out=h_codes[:].bitcast(FP8X4), scales=h_sc[:], in_=h_bf[g][:])
+            y[g, 0] = bank((4 + 2 * g) % 8, "y_first%d" % g, [P, P])[:]
+            rest = bank((5 + 2 * g) % 8, "y_rest%d" % g, [P, D - 1, P])
+            for d in range(1, D):
+                y[g, d] = rest[:, d - 1, :]
             for d in range(D):
                 nc.tensor.matmul_mx(
-                    out=y[i, d],
+                    out=y[g, d],
                     lhsT=ep_w[:, d * V : (d + 1) * V].bitcast(FP8X4),
                     lhsT_scale=e_plane[:, d * V : (d + 1) * V],
                     rhs=h_codes[:].bitcast(FP8X4),
@@ -168,25 +162,24 @@ def tile_picked_ycham_root_p_kernel(tc, x_words, x_scales, w1, e_words, e_scales
                 )
 
         top = {}
-        for i, (g0, n) in enumerate(pieces):
-            top[i, 0] = sb("top%d0" % i, [P, n * P], F32)
-            nc.scalar.activation(top[i, 0][:], y[i, 0], ACT.Identity, bias=neg_nb[:, 0:1])
-        for i, d in [(0, 1), (1, 1), (0, 2), (2, 1), (1, 2), (0, 3), (3, 1), (2, 2), (1, 3), (3, 2), (2, 3), (3, 3)]:
-            n = pieces[i][1]
-            top[i, d] = sb("top%d%d" % (i, d), [P, n * P], F32)
-            for part in [slice(0, n * P)] if d < D - 1 else [slice(a * P, (a + 1) * P) for a in range(n)]:
-                nc.vector.scalar_tensor_tensor(top[i, d][:, part], y[i, d][:, part], neg_nb[:, d : d + 1], top[i, d - 1][:, part], ALU.add, ALU.max)
+        for g in range(GROUPS):
+            top[g, 0] = sb("top%d0" % g, [P, P], F32)
+            nc.scalar.activation(top[g, 0][:], y[g, 0], ACT.Identity, bias=neg_nb[:, 0:1])
+        for diagonal in range(1, GROUPS + D - 1):
+            for d in range(1, D):
+                g = diagonal - d
+                if 0 <= g < GROUPS:
+                    top[g, d] = sb("top%d%d" % (g, d), [P, P], F32)
+                    nc.vector.scalar_tensor_tensor(top[g, d][:], y[g, d], neg_nb[:, d : d + 1], top[g, d - 1][:], ALU.add, ALU.max)
 
-        for g in range(4):
-            i = piece_of[g]
-            a = g - pieces[i][0]
+        for g in range(GROUPS):
             rr = sb("rr%d" % g, [P, V], F32)
             res = sb("res%d" % g, [P, V], F32)
             o_ps = bank((4 + 2 * g) % 8, "o_ps%d" % g, [P, V])
-            nc.tensor.transpose(o_ps[:], top[i, D - 1][:, a * P : (a + 1) * P], ident[:])
-            if g < 2:
+            nc.tensor.transpose(o_ps[:], top[g, D - 1][:], ident[:])
+            if g < SCALAR_CLAMPS:
                 nc.scalar.activation(rr[:], o_ps[:], ACT.Relu, bias=own_t[:, g : g + 1], scale=-1.0)
             else:
                 nc.vector.tensor_scalar(rr[:], o_ps[:], own_t[:, g : g + 1], 0.0, ALU.subtract, ALU.min)
-            nc.scalar.activation(res[:], rr[:], ACT.Sqrt, bias=eps[:], scale=1.0 if g < 2 else -1.0)
-            (nc.scalar if g == 3 else nc.sync).dma_start(out[g * P : (g + 1) * P, :], res[:])
+            nc.scalar.activation(res[:], rr[:], ACT.Sqrt, bias=eps[:], scale=1.0 if g < SCALAR_CLAMPS else -1.0)
+            (nc.scalar if g == GROUPS - 1 else nc.sync).dma_start(out[g * P : (g + 1) * P, :], res[:])

@@ -82,104 +82,136 @@ def tile_picked_ycham_root_p_kernel(tc, x_words, x_scales, w1, e_words, e_scales
         nc.sync.dma_start(w_raw[:, 1:PACK, :], w_rows[:, 1:PACK, :])
         nc.sync.dma_start(xw[:], x_words[0].rearrange("p n t -> p (n t)").bitcast(I32))
 
-        xg_s = at("xg_s", [P, S], U8, X_HOLD + 4 * H - S // 2)
+        xg_s = at("xg_s", [P, S], U8, X_HOLD + 2 * H - S // 2)
         nc.vector.tensor_copy(xg_s[:], xs[:].indirect(offs_t[:]))
         for r in range(4):
             nc.sync.dma_start(x_plane[r:P:32, :].bitcast(I32), xg_s[X_FIRST + r : X_FIRST + ROWS : 4, :].bitcast(I32))
         ew = at("ew", [P, W], I32, 0)
         nc.sync.dma_start(ew[:], e_words[0].rearrange("p n t -> p (n t)").bitcast(I32))
 
-        eg_s = sb("eg_s", [P, U], U8)
-        nc.vector.tensor_copy(eg_s[:], es[:].indirect(oth_t[:]))
         ep_s = at("ep_s", [P, U], U8, E_HOLD)
-        nc.vector.tensor_copy(ep_s[:].rearrange("p (d v) -> p d v", d=D), eg_s[:].rearrange("p (v d) -> p d v", d=D))
+        nc.vector.tensor_copy(ep_s[:].rearrange("p (s v e) -> p v s e", s=2, e=2), es[:].indirect(oth_t[:]))
         for r in range(4):
             nc.sync.dma_start(e_plane[r:P:32, :].bitcast(I32), ep_s[E_FIRST + r : E_FIRST + ROWS : 4, :].bitcast(I32))
-        own_t = sb("own_t", [P, GROUPS], F32, tag="eg_s")
+        own_t = sb("own_t", [P, GROUPS], F32, tag="es")
         with nc.allow_non_contiguous_dma(reason="512 norms, one to a partition and group"):
             nc.sync.dma_start(own_t[:], own.rearrange("(g p) o -> p (g o)", g=GROUPS))
 
-        w_src = w_raw[:].rearrange("p j (m t) -> p t m j", t=PACK)
-        w_bf = []
-        for a in range(2):
-            w_pair = sb("w_pair%d" % a, [P, 2, PACK * P], BF16)
-            nc.scalar.copy(w_pair[:].rearrange("p t (m j) -> p m j t", j=PACK), w_src[:, 2 * a : 2 * a + 2].rearrange("p t m j -> p m j t"))
-            w_bf.extend([w_pair[:, 0, :], w_pair[:, 1, :]])
-
         nb_g = sb("nb_g", [P, U], F32)
-        nc.vector.tensor_copy(nb_g[:], nb_t[:].indirect(oth_t[:]))
+        nc.vector.tensor_copy(nb_g[:].rearrange("p (s v e) -> p v s e", s=2, e=2), nb_t[:].indirect(oth_t[:]))
         nb_ps = bank(7, "nb_ps", [P, D, P])
-        for d in range(D):
-            nc.tensor.transpose(nb_ps[:, d, :], nb_g[:, d : U : D], ident[:])
+        for u in range(D):
+            nc.tensor.transpose(nb_ps[:, u, :], nb_g[:, u * P : (u + 1) * P], ident[:])
+
+        w_src = w_raw[:].rearrange("p j (m t) -> p t m j", t=PACK)
+        w_low = sb("w_low", [P, 2, PACK * P], BF16)
+        nc.scalar.copy(w_low[:].rearrange("p t (m j) -> p m j t", j=PACK), w_src[:, 0:2].rearrange("p t m j -> p m j t"))
+        w_high = sb("w_high", [P, 2, PACK * P], BF16)
+        high = w_high[:].rearrange("p t (m j) -> p t m j", j=PACK)
+        nc.scalar.copy(high[:, :, 0:64].rearrange("p t m j -> p m j t"), w_src[:, 2:4, 0:64].rearrange("p t m j -> p m j t"))
+        nc.vector.tensor_copy(high[:, :, 64:P], w_src[:, 2:4, 64:P])
+        w_codes = [sb("w_codes0", [P, 2 * P], U32), at("w_codes1", [P, 2 * P], U32, X_HOLD)]
+        w_sc = sb("w_sc", [P, H], U8)
+        xg_first = sb("xg_first", [P, P], U32)
+        xg_rest = at("xg_rest", [P, S - P], U32, X_HOLD + 2 * H)
+        xg_w = [xg_first[:]] + [xg_rest[:, g * P : (g + 1) * P] for g in range(GROUPS - 1)]
+        for a, w_bf in enumerate([w_low, w_high]):
+            nc.vector.quantize_mx(out=w_codes[a][:].bitcast(FP8X4), scales=w_sc[:, 2 * a * P : 2 * (a + 1) * P], in_=w_bf[:].rearrange("p t n -> p (t n)"))
         neg_nb = sb("neg_nb", [P, D], F32, tag="w_raw")
         nc.scalar.activation(neg_nb[:], nb_ps[:, :, NB_ROW], ACT.Copy, scale=-1.0)
 
-        xg_w = [sb("xg_w0", [P, HALF], U32)]
-        nc.vector.tensor_copy(xg_w[0][:], xw[:].bitcast(U32).indirect(offs_t[:, 0 : HALF // 16]))
-        w_codes = at("w_codes", [P, H], U32, X_HOLD)
-        w_sc = sb("w_sc", [P, H], U8)
-        for t in range(PACK):
-            nc.vector.quantize_mx(out=w_codes[:, t * P : (t + 1) * P].bitcast(FP8X4), scales=w_sc[:, t * P : (t + 1) * P], in_=w_bf[t])
-        xg_w.append(at("xg_w1", [P, HALF], U32, X_HOLD + 4 * H))
-        nc.vector.tensor_copy(xg_w[1][:], xw[:].bitcast(U32).indirect(offs_t[:, HALF // 16 : S // 16]))
-
-        h_bf = [at("h_bf%d" % g, [P, PACK * P], BF16, H_AT + 2 * PACK * P * g) for g in range(GROUPS)]
+        h_bf = [at("h_bf%d" % c, [P, 2, PACK * P], BF16, H_AT + 4 * PACK * P * c) for c in range(2)]
         for g in range(GROUPS):
+            nc.vector.tensor_copy(xg_w[g], xw[:].bitcast(U32).indirect(offs_t[:, 8 * g : 8 * (g + 1)]))
             h_ps = bank(g, "h_ps%d" % g, [P, PACK, P])
             for t in range(PACK):
                 nc.tensor.matmul_mx(
                     out=h_ps[:, t, :],
-                    lhsT=w_codes[:, t * P : (t + 1) * P].bitcast(FP8X4),
+                    lhsT=w_codes[t // 2][:, (t % 2) * P : (t % 2 + 1) * P].bitcast(FP8X4),
                     lhsT_scale=w_sc[:, t * P : (t + 1) * P],
-                    rhs=xg_w[g // 2][:, (g % 2) * P : (g % 2 + 1) * P].bitcast(FP8X4),
+                    rhs=xg_w[g].bitcast(FP8X4),
                     rhs_scale=x_plane[:, g * P : (g + 1) * P],
                     start=True,
                     stop=True,
                 )
-            nc.scalar.copy(h_bf[g][:].rearrange("p (n t) -> p n t", t=PACK), h_ps[:].rearrange("p t n -> p n t"))
+            nc.scalar.copy(h_bf[g // 2][:, g % 2, :].rearrange("p (n t) -> p n t", t=PACK), h_ps[:].rearrange("p t n -> p n t"))
 
-        ep_w = sb("ep_w", [P, U], U32)
-        nc.vector.tensor_copy(ep_w[:].rearrange("p (d v) -> p v d", d=D), ew[:].bitcast(U32).indirect(oth_t[:]))
+        chunks = [(0, 1, [4, 5, 6, 7]), (1, 1, [0, 1]), (2, 1, [2, 4]), (3, 1, [3, 6])]
+        ep_w = [sb("ep_w0", [P, U // 2], U32), at("ep_w1", [P, U // 2], U32, E_HOLD + U - 64)]
+        h_codes = sb("h_codes", [P, S], U32)
+        h_sc = {}
 
-        y = {}
-        for g in range(GROUPS):
-            h_codes = sb("h_codes%d" % g, [P, P], U32)
-            h_sc = at("h_sc%d" % g, [P, P], U8, E_HOLD + g * P)
-            nc.vector.quantize_mx(out=h_codes[:].bitcast(FP8X4), scales=h_sc[:], in_=h_bf[g][:])
-            y[g, 0] = bank((4 + 2 * g) % 8, "y_first%d" % g, [P, P])[:]
-            rest = bank((5 + 2 * g) % 8, "y_rest%d" % g, [P, D - 1, P])
-            for d in range(1, D):
-                y[g, d] = rest[:, d - 1, :]
-            for d in range(D):
+        def gather_e(a):
+            nc.vector.tensor_copy(ep_w[a][:].rearrange("p (s v e) -> p v s e", s=2, e=2), ew[:].bitcast(U32).indirect(oth_t[:, a * 16 : (a + 1) * 16]))
+
+        def quantise(c):
+            g, n, banks = chunks[c]
+            h_sc[c] = at("h_sc%d" % c, [P, n * P], U8, E_HOLD + g * P - 64)
+            src = h_bf[g // 2][:, g % 2 : g % 2 + n, :].rearrange("p g n -> p (g n)")
+            nc.vector.quantize_mx(out=h_codes[:, g * P : (g + n) * P].bitcast(FP8X4), scales=h_sc[c][:], in_=src)
+
+        pair = {}
+
+        def product(c):
+            g, n, banks = chunks[c]
+            y = {}
+            if len(banks) == 4:
+                order = [(a, s) for a in range(2) for s in range(2)]
+                for a, s in order:
+                    y[a, s] = bank(banks[2 * a + s], "y%d%d%d" % (c, a, s), [P, n * P])[:]
+            else:
+                order = [(a, s) for s in range(2) for a in range(2)]
+                for s in range(2):
+                    both = bank(banks[s], "y%d%d" % (c, s), [P, 2, n * P])
+                    for a in range(2):
+                        y[a, s] = both[:, a, :]
+            for a, s in order:
                 nc.tensor.matmul_mx(
-                    out=y[g, d],
-                    lhsT=ep_w[:, d * V : (d + 1) * V].bitcast(FP8X4),
-                    lhsT_scale=e_plane[:, d * V : (d + 1) * V],
-                    rhs=h_codes[:].bitcast(FP8X4),
-                    rhs_scale=h_sc[:],
+                    out=y[a, s],
+                    lhsT=ep_w[a][:, s * P : (s + 1) * P].bitcast(FP8X4),
+                    lhsT_scale=e_plane[:, (2 * s + a) * P : (2 * s + a + 1) * P],
+                    rhs=h_codes[:, g * P : (g + n) * P].bitcast(FP8X4),
+                    rhs_scale=h_sc[c][:],
                     start=True,
                     stop=True,
                 )
+            for a in range(2):
+                low = sb("low%d%d" % (c, a), [P, n * P], F32)
+                nc.scalar.activation(low[:], y[a, 0], ACT.Identity, bias=neg_nb[:, a : a + 1])
+                both = sb("pair%d%d" % (c, a), [P, n * P], F32)
+                nc.vector.scalar_tensor_tensor(both[:], y[a, 1], neg_nb[:, 2 + a : 3 + a], low[:], ALU.add, ALU.max)
+                for i in range(n):
+                    pair[g + i, a] = both[:, i * P : (i + 1) * P]
 
-        top = {}
-        for g in range(GROUPS):
-            top[g, 0] = sb("top%d0" % g, [P, P], F32)
-            nc.scalar.activation(top[g, 0][:], y[g, 0], ACT.Identity, bias=neg_nb[:, 0:1])
-        for diagonal in range(1, GROUPS + D - 1):
-            for d in range(1, D):
-                g = diagonal - d
-                if 0 <= g < GROUPS:
-                    top[g, d] = sb("top%d%d" % (g, d), [P, P], F32)
-                    nc.vector.scalar_tensor_tensor(top[g, d][:], y[g, d], neg_nb[:, d : d + 1], top[g, d - 1][:], ALU.add, ALU.max)
+        o_ps = {}
 
-        for g in range(GROUPS):
+        def turn(groups, b):
+            turned = bank(b, "o_ps%d" % b, [P, len(groups), 2, P])
+            for i, g in enumerate(groups):
+                o_ps[g] = turned[:, i]
+                for a in range(2):
+                    nc.tensor.transpose(turned[:, i, a, :], pair[g, a], ident[:])
+
+        def finish(g):
+            top = sb("top%d" % g, [P, V], F32)
             rr = sb("rr%d" % g, [P, V], F32)
             res = sb("res%d" % g, [P, V], F32)
-            o_ps = bank((4 + 2 * g) % 8, "o_ps%d" % g, [P, V])
-            nc.tensor.transpose(o_ps[:], top[g, D - 1][:], ident[:])
-            if g < SCALAR_CLAMPS:
-                nc.scalar.activation(rr[:], o_ps[:], ACT.Relu, bias=own_t[:, g : g + 1], scale=-1.0)
+            nc.vector.tensor_reduce(top[:], o_ps[g].rearrange("p a (v e) -> p (a v) e", e=2), mybir.AxisListType.X, ALU.max)
+            if g < 4:
+                nc.scalar.activation(rr[:], top[:], ACT.Relu, bias=own_t[:, g : g + 1], scale=-1.0)
             else:
-                nc.vector.tensor_scalar(rr[:], o_ps[:], own_t[:, g : g + 1], 0.0, ALU.subtract, ALU.min)
-            nc.scalar.activation(res[:], rr[:], ACT.Sqrt, bias=eps[:], scale=1.0 if g < SCALAR_CLAMPS else -1.0)
+                nc.vector.tensor_scalar(rr[:], top[:], own_t[:, g : g + 1], 0.0, ALU.subtract, ALU.min)
+            nc.scalar.activation(res[:], rr[:], ACT.Sqrt, bias=eps[:], scale=1.0 if g < 4 else -1.0)
             (nc.scalar if g == GROUPS - 1 else nc.sync).dma_start(out[g * P : (g + 1) * P, :], res[:])
+
+        gather_e(0)
+        quantise(0)
+        gather_e(1)
+        for c in range(1, len(chunks)):
+            quantise(c)
+        for c in range(len(chunks)):
+            product(c)
+        for g in range(GROUPS):
+            turn([g], [5, 7, 0, 1][g])
+        for g in range(GROUPS):
+            finish(g)

@@ -108,8 +108,8 @@ def tile_picked_ycham_root_p_kernel(tc, x_words, x_scales, w1, e_words, e_scales
         nc.scalar.copy(w_low[:].rearrange("p t (m j) -> p m j t", j=PACK), w_src[:, 0:2].rearrange("p t m j -> p m j t"))
         w_high = sb("w_high", [P, 2, PACK * P], BF16)
         high = w_high[:].rearrange("p t (m j) -> p t m j", j=PACK)
-        nc.scalar.copy(high[:, :, 0:64].rearrange("p t m j -> p m j t"), w_src[:, 2:4, 0:64].rearrange("p t m j -> p m j t"))
-        nc.vector.tensor_copy(high[:, :, 64:P], w_src[:, 2:4, 64:P])
+        nc.scalar.copy(high[:, :, 0:32].rearrange("p t m j -> p m j t"), w_src[:, 2:4, 0:32].rearrange("p t m j -> p m j t"))
+        nc.vector.tensor_copy(high[:, :, 32:P], w_src[:, 2:4, 32:P])
         w_codes = [sb("w_codes0", [P, 2 * P], U32), at("w_codes1", [P, 2 * P], U32, X_HOLD)]
         w_sc = sb("w_sc", [P, H], U8)
         xg_first = sb("xg_first", [P, P], U32)
@@ -197,11 +197,11 @@ def tile_picked_ycham_root_p_kernel(tc, x_words, x_scales, w1, e_words, e_scales
             rr = sb("rr%d" % g, [P, V], F32)
             res = sb("res%d" % g, [P, V], F32)
             nc.vector.tensor_reduce(top[:], o_ps[g].rearrange("p a (v e) -> p (a v) e", e=2), mybir.AxisListType.X, ALU.max)
-            if g < 4:
+            if g < 3:
                 nc.scalar.activation(rr[:], top[:], ACT.Relu, bias=own_t[:, g : g + 1], scale=-1.0)
             else:
                 nc.vector.tensor_scalar(rr[:], top[:], own_t[:, g : g + 1], 0.0, ALU.subtract, ALU.min)
-            nc.scalar.activation(res[:], rr[:], ACT.Sqrt, bias=eps[:], scale=1.0 if g < 4 else -1.0)
+            nc.scalar.activation(res[:], rr[:], ACT.Sqrt, bias=eps[:], scale=1.0 if g < 3 else -1.0)
             (nc.scalar if g == GROUPS - 1 else nc.sync).dma_start(out[g * P : (g + 1) * P, :], res[:])
 
         gather_e(0)

@@ -185,23 +185,26 @@ def tile_picked_ycham_root_p_kernel(tc, x_words, x_scales, w1, e_words, e_scales
 
         o_ps = {}
 
-        def turn(groups, b):
-            turned = bank(b, "o_ps%d" % b, [P, len(groups), 2, P])
-            for i, g in enumerate(groups):
-                o_ps[g] = turned[:, i]
-                for a in range(2):
-                    nc.tensor.transpose(turned[:, i, a, :], pair[g, a], ident[:])
+        def turn(g, banks):
+            n = 2 // len(banks)
+            o_ps[g] = []
+            for i, b in enumerate(banks):
+                turned = bank(b, "o_ps%d" % b, [P, n, P])
+                for a in range(n):
+                    nc.tensor.transpose(turned[:, a, :], pair[g, i + a], ident[:])
+                o_ps[g].append((turned[:].rearrange("p a (v e) -> p (a v) e", e=2), slice(i * 64, (i + n) * 64)))
 
         def finish(g):
             top = sb("top%d" % g, [P, V], F32)
             rr = sb("rr%d" % g, [P, V], F32)
             res = sb("res%d" % g, [P, V], F32)
-            nc.vector.tensor_reduce(top[:], o_ps[g].rearrange("p a (v e) -> p (a v) e", e=2), mybir.AxisListType.X, ALU.max)
-            if g < 3:
+            for view, cols in o_ps[g]:
+                nc.vector.tensor_reduce(top[:, cols], view, mybir.AxisListType.X, ALU.max)
+            if g < SCALAR_CLAMPS:
                 nc.scalar.activation(rr[:], top[:], ACT.Relu, bias=own_t[:, g : g + 1], scale=-1.0)
             else:
                 nc.vector.tensor_scalar(rr[:], top[:], own_t[:, g : g + 1], 0.0, ALU.subtract, ALU.min)
-            nc.scalar.activation(res[:], rr[:], ACT.Sqrt, bias=eps[:], scale=1.0 if g < 3 else -1.0)
+            nc.scalar.activation(res[:], rr[:], ACT.Sqrt, bias=eps[:], scale=1.0 if g < SCALAR_CLAMPS else -1.0)
             (nc.scalar if g == GROUPS - 1 else nc.sync).dma_start(out[g * P : (g + 1) * P, :], res[:])
 
         gather_e(0)
@@ -212,6 +215,6 @@ def tile_picked_ycham_root_p_kernel(tc, x_words, x_scales, w1, e_words, e_scales
         for c in range(len(chunks)):
             product(c)
         for g in range(GROUPS):
-            turn([g], [5, 7, 0, 1][g])
+            turn(g, [[5], [7], [0], [1, 4]][g])
         for g in range(GROUPS):
             finish(g)

@@ -29,6 +29,7 @@ SCALAR_CLAMPS = 2
 H_AT = 4 * W + 8 * P
 X_HOLD = 16384
 E_HOLD = 24576
+STEP_HOLD = 32768
 
 
 def tile_picked_ycham_root_p_kernel(tc, x_words, x_scales, w1, e_words, e_scales, nb, own, offs, oth, out):
@@ -119,6 +120,8 @@ def tile_picked_ycham_root_p_kernel(tc, x_words, x_scales, w1, e_words, e_scales
             nc.vector.quantize_mx(out=w_codes[a][:].bitcast(FP8X4), scales=w_sc[:, 2 * a * P : 2 * (a + 1) * P], in_=w_bf[:].rearrange("p t n -> p (t n)"))
         neg_nb = sb("neg_nb", [P, D], F32, tag="w_raw")
         nc.scalar.activation(neg_nb[:], nb_ps[:, :, NB_ROW], ACT.Copy, scale=-1.0)
+        neg_first = at("neg_first", [P, 1], F32, STEP_HOLD)
+        nc.scalar.activation(neg_first[:], nb_ps[:, 0:1, NB_ROW], ACT.Copy, scale=-1.0)
 
         h_bf = [at("h_bf%d" % c, [P, 2, PACK * P], BF16, H_AT + 4 * PACK * P * c) for c in range(2)]
         for g in range(GROUPS):
@@ -146,7 +149,7 @@ def tile_picked_ycham_root_p_kernel(tc, x_words, x_scales, w1, e_words, e_scales
 
         def quantise(c):
             g, n, banks = chunks[c]
-            h_sc[c] = at("h_sc%d" % c, [P, n * P], U8, E_HOLD + g * P - 64)
+            h_sc[c] = at("h_sc%d" % c, [P, n * P], U8, E_HOLD + g * P - 64 if g < GROUPS - 1 else STEP_HOLD)
             src = h_bf[g // 2][:, g % 2 : g % 2 + n, :].rearrange("p g n -> p (g n)")
             nc.vector.quantize_mx(out=h_codes[:, g * P : (g + n) * P].bitcast(FP8X4), scales=h_sc[c][:], in_=src)
 
@@ -175,9 +178,16 @@ def tile_picked_ycham_root_p_kernel(tc, x_words, x_scales, w1, e_words, e_scales
                     start=True,
                     stop=True,
                 )
+            if c == 0:
+                first = at("low00", [P, P], F32, H_AT)
+                nc.vector.tensor_scalar(first[:], y[0, 0], neg_first[:], None, ALU.add)
+                quantise(GROUPS - 1)
             for a in range(2):
-                low = sb("low%d%d" % (c, a), [P, n * P], F32)
-                nc.scalar.activation(low[:], y[a, 0], ACT.Identity, bias=neg_nb[:, a : a + 1])
+                if c == 0 and a == 0:
+                    low = first
+                else:
+                    low = sb("low%d%d" % (c, a), [P, n * P], F32)
+                    nc.scalar.activation(low[:], y[a, 0], ACT.Identity, bias=neg_nb[:, a : a + 1])
                 both = sb("pair%d%d" % (c, a), [P, n * P], F32)
                 nc.vector.scalar_tensor_tensor(both[:], y[a, 1], neg_nb[:, 2 + a : 3 + a], low[:], ALU.add, ALU.max)
                 for i in range(n):
@@ -210,7 +220,7 @@ def tile_picked_ycham_root_p_kernel(tc, x_words, x_scales, w1, e_words, e_scales
         gather_e(0)
         quantise(0)
         gather_e(1)
-        for c in range(1, len(chunks)):
+        for c in range(1, len(chunks) - 1):
             quantise(c)
         for c in range(len(chunks)):
             product(c)

@@ -25,6 +25,7 @@ ROWS = 16
 X_FIRST = 112
 E_FIRST = 48
 NB_ROW = P - 1
+BOTH_CLAMPED = 1
 SCALAR_CLAMPS = 2
 H_AT = 4 * W + 8 * P
 X_HOLD = 16384
@@ -205,16 +206,24 @@ def tile_picked_ycham_root_p_kernel(tc, x_words, x_scales, w1, e_words, e_scales
                 o_ps[g].append((turned[:].rearrange("p a (v e) -> p (a v) e", e=2), slice(i * 64, (i + n) * 64)))
 
         def finish(g):
-            top = sb("top%d" % g, [P, V], F32)
+            top = sb("top%d" % g, [P, V], F32) if g >= BOTH_CLAMPED else None
             rr = sb("rr%d" % g, [P, V], F32)
             res = sb("res%d" % g, [P, V], F32)
-            for view, cols in o_ps[g]:
+            if g < BOTH_CLAMPED:
+                two = sb("two%d" % g, [P, 2, V], F32)
+                nc.scalar.activation(two[:], o_ps[g][0][0].rearrange("p v e -> p e v"), ACT.Relu, bias=own_t[:, g : g + 1], scale=-1.0)
+                nc.vector.tensor_tensor(rr[:], two[:, 0, :], two[:, 1, :], ALU.min)
+            for view, cols in o_ps[g] if g >= BOTH_CLAMPED else []:
                 nc.vector.tensor_reduce(top[:, cols], view, mybir.AxisListType.X, ALU.max)
-            if g < SCALAR_CLAMPS:
+            if g < BOTH_CLAMPED:
+                pass
+            elif g < SCALAR_CLAMPS:
                 nc.scalar.activation(rr[:], top[:], ACT.Relu, bias=own_t[:, g : g + 1], scale=-1.0)
             else:
-                nc.vector.tensor_scalar(rr[:], top[:], own_t[:, g : g + 1], 0.0, ALU.subtract, ALU.min)
-            nc.scalar.activation(res[:], rr[:], ACT.Sqrt, bias=eps[:], scale=1.0 if g < SCALAR_CLAMPS else -1.0)
+                for view, cols in o_ps[g]:
+                    nc.vector.tensor_scalar(rr[:, cols], top[:, cols], own_t[:, g : g + 1], 0.0, ALU.subtract, ALU.min)
+            for view, cols in o_ps[g]:
+                nc.scalar.activation(res[:, cols], rr[:, cols], ACT.Sqrt, bias=eps[:], scale=1.0 if g < SCALAR_CLAMPS else -1.0)
             (nc.scalar if g == GROUPS - 1 else nc.sync).dma_start(out[g * P : (g + 1) * P, :], res[:])
 
         gather_e(0)

@@ -30,7 +30,6 @@ SCALAR_CLAMPS = 2
 H_AT = 4 * W + 8 * P
 X_HOLD = 16384
 E_HOLD = 24576
-STEP_HOLD = 32768
 
 
 def tile_picked_ycham_root_p_kernel(tc, x_words, x_scales, w1, e_words, e_scales, nb, own, offs, oth, out):
@@ -121,8 +120,6 @@ def tile_picked_ycham_root_p_kernel(tc, x_words, x_scales, w1, e_words, e_scales
             nc.vector.quantize_mx(out=w_codes[a][:].bitcast(FP8X4), scales=w_sc[:, 2 * a * P : 2 * (a + 1) * P], in_=w_bf[:].rearrange("p t n -> p (t n)"))
         neg_nb = sb("neg_nb", [P, D], F32, tag="w_raw")
         nc.scalar.activation(neg_nb[:], nb_ps[:, :, NB_ROW], ACT.Copy, scale=-1.0)
-        neg_first = at("neg_first", [P, 1], F32, STEP_HOLD)
-        nc.scalar.activation(neg_first[:], nb_ps[:, 0:1, NB_ROW], ACT.Copy, scale=-1.0)
 
         h_bf = [at("h_bf%d" % c, [P, 2, PACK * P], BF16, H_AT + 4 * PACK * P * c) for c in range(2)]
         for g in range(GROUPS):
@@ -150,7 +147,7 @@ def tile_picked_ycham_root_p_kernel(tc, x_words, x_scales, w1, e_words, e_scales
 
         def quantise(c):
             g, n, banks = chunks[c]
-            h_sc[c] = at("h_sc%d" % c, [P, n * P], U8, E_HOLD + g * P - 64 if g < GROUPS - 1 else STEP_HOLD)
+            h_sc[c] = at("h_sc%d" % c, [P, n * P], U8, E_HOLD + g * P - 64)
             src = h_bf[g // 2][:, g % 2 : g % 2 + n, :].rearrange("p g n -> p (g n)")
             nc.vector.quantize_mx(out=h_codes[:, g * P : (g + n) * P].bitcast(FP8X4), scales=h_sc[c][:], in_=src)
 
@@ -179,16 +176,9 @@ def tile_picked_ycham_root_p_kernel(tc, x_words, x_scales, w1, e_words, e_scales
                     start=True,
                     stop=True,
                 )
-            if c == 0:
-                first = at("low00", [P, P], F32, H_AT)
-                nc.vector.tensor_scalar(first[:], y[0, 0], neg_first[:], None, ALU.add)
-                quantise(GROUPS - 1)
             for a in range(2):
-                if c == 0 and a == 0:
-                    low = first
-                else:
-                    low = sb("low%d%d" % (c, a), [P, n * P], F32)
-                    nc.scalar.activation(low[:], y[a, 0], ACT.Identity, bias=neg_nb[:, a : a + 1])
+                low = sb("low%d%d" % (c, a), [P, n * P], F32)
+                nc.scalar.activation(low[:], y[a, 0], ACT.Identity, bias=neg_nb[:, a : a + 1])
                 both = sb("pair%d%d" % (c, a), [P, n * P], F32)
                 nc.vector.scalar_tensor_tensor(both[:], y[a, 1], neg_nb[:, 2 + a : 3 + a], low[:], ALU.add, ALU.max)
                 for i in range(n):
@@ -229,7 +219,7 @@ def tile_picked_ycham_root_p_kernel(tc, x_words, x_scales, w1, e_words, e_scales
         gather_e(0)
         quantise(0)
         gather_e(1)
-        for c in range(1, len(chunks) - 1):
+        for c in range(1, len(chunks)):
             quantise(c)
         for c in range(len(chunks)):
             product(c)

from contextlib import ExitStack

import concourse.mybir as mybir
from concourse.masks import make_identity

K, T, S, H, D, W, U = 512, 2048, 512, 512, 4, 2048, 512
P = 128
V = U // D
FLOPS = 2 * K * H * S + 2 * H * S * U

F32 = mybir.dt.float32
BF16 = mybir.dt.bfloat16
I32 = mybir.dt.int32
U32 = mybir.dt.uint32
U16 = mybir.dt.uint16
U8 = mybir.dt.uint8
FP8X4 = mybir.dt.float8_e4m3fn_x4
ALU = mybir.AluOpType
ACT = mybir.ActivationFunctionType

PACK = 4
GROUPS = S // P
HALF = S // 2
ROWS = 16
X_FIRST = 112
E_FIRST = 48
NB_ROW = P - 1
BOTH_CLAMPED = 1
SCALAR_CLAMPS = 2
H_AT = 4 * W + 8 * P
X_HOLD = 16384
E_HOLD = 24576


def tile_picked_ycham_root_p_kernel(tc, x_words, x_scales, w1, e_words, e_scales, nb, own, offs, oth, out):
    nc = tc.nc
    with ExitStack() as ctx:
        keep = ctx.enter_context(tc.tile_pool(name="keep", bufs=1))
        placed = ctx.enter_context(tc.tile_pool(name="placed", bufs=1))
        psum = ctx.enter_context(tc.psum_pool(name="psum", bufs=1))

        def sb(name, shape, dtype, tag=None):
            return keep.tile(shape, dtype, name=name, tag=tag or name, align_bytes=64)

        def at(name, shape, dtype, offset):
            return placed.tile(shape, dtype, name=name, tag=name, align_bytes=64, offset=offset)

        def bank(b, name, shape):
            return psum.tile(shape, F32, name=name, tag="bank%d" % b)

        offs_t = sb("offs_t", [P, S // 16], U16)
        oth_t = sb("oth_t", [P, U // 16], U16)
        es = sb("es", [P, W], U8)
        nb_t = sb("nb_t", [P, W], F32)
        w_raw = sb("w_raw", [P, PACK, H], F32)
        eps = sb("eps", [P, 1], F32)
        one = sb("one", [P, 1], F32)
        ident = sb("ident", [P, P], F32)
        xs = at("xs", [P, T], U8, 0)
        x_plane = sb("x_plane", [P, S], U8)
        e_plane = sb("e_plane", [P, U], U8)
        xw = sb("xw", [P, T], I32)

        nc.scalar.dma_start(xs[X_FIRST : X_FIRST + ROWS, :].bitcast(I32), x_scales[0].bitcast(I32))

        nc.vector.memset(one[:], 1.0)
        nc.vector.memset(ident[:], 0.0)
        nc.vector.memset(xs[0:X_FIRST, :].bitcast(I32), 0)
        nc.vector.memset(es[0:E_FIRST, :].bitcast(I32), 0)
        nc.vector.memset(es[E_FIRST + ROWS : P, :].bitcast(I32), 0)
        nc.vector.memset(x_plane[:].bitcast(I32), 0)
        nc.vector.memset(e_plane[:].bitcast(I32), 0)
        make_identity(nc, ident[:], nomemset=True)
        nc.scalar.activation(eps[:], one[:], ACT.Sqrt, scale=1e-4)
        nc.scalar.activation(nb_t[0:NB_ROW, :], eps[0:NB_ROW, :].to_broadcast([NB_ROW, W]), ACT.Copy, scale=0.0)
        w_rows = w1.rearrange("(p j) c -> p j c", j=PACK)

        nc.sync.dma_start(offs_t[:], offs)
        nc.sync.dma_start(w_raw[:, 0:1, :], w_rows[:, 0:1, :])
        nc.sync.dma_start(oth_t[:], oth)
        nc.sync.dma_start(es[E_FIRST : E_FIRST + ROWS, :].bitcast(I32), e_scales[0].bitcast(I32))
        nc.sync.dma_start(nb_t[NB_ROW : NB_ROW + 1, :], nb[0:1, :])
        nc.sync.dma_start(w_raw[:, 1:PACK, :], w_rows[:, 1:PACK, :])
        nc.sync.dma_start(xw[:], x_words[0].rearrange("p n t -> p (n t)").bitcast(I32))

        xg_s = at("xg_s", [P, S], U8, X_HOLD + 2 * H - S // 2)
        nc.vector.tensor_copy(xg_s[:], xs[:].indirect(offs_t[:]))
        for r in range(4):
            nc.sync.dma_start(x_plane[r:P:32, :].bitcast(I32), xg_s[X_FIRST + r : X_FIRST + ROWS : 4, :].bitcast(I32))
        ew = at("ew", [P, W], I32, 0)
        nc.sync.dma_start(ew[:], e_words[0].rearrange("p n t -> p (n t)").bitcast(I32))

        ep_s = at("ep_s", [P, U], U8, E_HOLD)
        nc.vector.tensor_copy(ep_s[:].rearrange("p (s v e) -> p v s e", s=2, e=2), es[:].indirect(oth_t[:]))
        for r in range(4):
            nc.sync.dma_start(e_plane[r:P:32, :].bitcast(I32), ep_s[E_FIRST + r : E_FIRST + ROWS : 4, :].bitcast(I32))
        own_t = sb("own_t", [P, GROUPS], F32, tag="es")
        with nc.allow_non_contiguous_dma(reason="512 norms, one to a partition and group"):
            nc.sync.dma_start(own_t[:], own.rearrange("(g p) o -> p (g o)", g=GROUPS))

        nb_g = sb("nb_g", [P, U], F32)
        nc.vector.tensor_copy(nb_g[:].rearrange("p (s v e) -> p v s e", s=2, e=2), nb_t[:].indirect(oth_t[:]))
        nb_ps = bank(7, "nb_ps", [P, D, P])
        for u in range(D):
            nc.tensor.transpose(nb_ps[:, u, :], nb_g[:, u * P : (u + 1) * P], ident[:])

        w_src = w_raw[:].rearrange("p j (m t) -> p t m j", t=PACK)
        w_low = sb("w_low", [P, 2, PACK * P], BF16)
        nc.scalar.copy(w_low[:].rearrange("p t (m j) -> p m j t", j=PACK), w_src[:, 0:2].rearrange("p t m j -> p m j t"))
        w_high = sb("w_high", [P, 2, PACK * P], BF16)
        high = w_high[:].rearrange("p t (m j) -> p t m j", j=PACK)
        nc.scalar.copy(high[:, :, 0:32].rearrange("p t m j -> p m j t"), w_src[:, 2:4, 0:32].rearrange("p t m j -> p m j t"))
        nc.vector.tensor_copy(high[:, :, 32:P], w_src[:, 2:4, 32:P])
        w_codes = [sb("w_codes0", [P, 2 * P], U32), at("w_codes1", [P, 2 * P], U32, X_HOLD)]
        w_sc = sb("w_sc", [P, H], U8)
        xg_first = sb("xg_first", [P, P], U32)
        xg_rest = at("xg_rest", [P, S - P], U32, X_HOLD + 2 * H)
        xg_w = [xg_first[:]] + [xg_rest[:, g * P : (g + 1) * P] for g in range(GROUPS - 1)]
        for a, w_bf in enumerate([w_low, w_high]):
            nc.vector.quantize_mx(out=w_codes[a][:].bitcast(FP8X4), scales=w_sc[:, 2 * a * P : 2 * (a + 1) * P], in_=w_bf[:].rearrange("p t n -> p (t n)"))
        neg_nb = sb("neg_nb", [P, D], F32, tag="w_raw")
        nc.scalar.activation(neg_nb[:], nb_ps[:, :, NB_ROW], ACT.Copy, scale=-1.0)

        h_bf = [at("h_bf%d" % c, [P, 2, PACK * P], BF16, H_AT + 4 * PACK * P * c) for c in range(2)]
        for g in range(GROUPS):
            nc.vector.tensor_copy(xg_w[g], xw[:].bitcast(U32).indirect(offs_t[:, 8 * g : 8 * (g + 1)]))
            h_ps = bank(g, "h_ps%d" % g, [P, PACK, P])
            for t in range(PACK):
                nc.tensor.matmul_mx(
                    out=h_ps[:, t, :],
                    lhsT=w_codes[t // 2][:, (t % 2) * P : (t % 2 + 1) * P].bitcast(FP8X4),
                    lhsT_scale=w_sc[:, t * P : (t + 1) * P],
                    rhs=xg_w[g].bitcast(FP8X4),
                    rhs_scale=x_plane[:, g * P : (g + 1) * P],
                    start=True,
                    stop=True,
                )
            nc.scalar.copy(h_bf[g // 2][:, g % 2, :].rearrange("p (n t) -> p n t", t=PACK), h_ps[:].rearrange("p t n -> p n t"))

        chunks = [(0, 1, [4, 5, 6, 7]), (1, 1, [0, 1]), (2, 1, [2, 4]), (3, 1, [3, 6])]
        ep_w = [sb("ep_w0", [P, U // 2], U32), at("ep_w1", [P, U // 2], U32, E_HOLD + U - 64)]
        h_codes = sb("h_codes", [P, S], U32)
        h_sc = {}

        def gather_e(a):
            nc.vector.tensor_copy(ep_w[a][:].rearrange("p (s v e) -> p v s e", s=2, e=2), ew[:].bitcast(U32).indirect(oth_t[:, a * 16 : (a + 1) * 16]))

        def quantise(c):
            g, n, banks = chunks[c]
            h_sc[c] = at("h_sc%d" % c, [P, n * P], U8, E_HOLD + g * P - 64)
            src = h_bf[g // 2][:, g % 2 : g % 2 + n, :].rearrange("p g n -> p (g n)")
            nc.vector.quantize_mx(out=h_codes[:, g * P : (g + n) * P].bitcast(FP8X4), scales=h_sc[c][:], in_=src)

        pair = {}

        def product(c):
            g, n, banks = chunks[c]
            y = {}
            if len(banks) == 4:
                order = [(a, s) for a in range(2) for s in range(2)]
                for a, s in order:
                    y[a, s] = bank(banks[2 * a + s], "y%d%d%d" % (c, a, s), [P, n * P])[:]
            else:
                order = [(a, s) for s in range(2) for a in range(2)]
                for s in range(2):
                    both = bank(banks[s], "y%d%d" % (c, s), [P, 2, n * P])
                    for a in range(2):
                        y[a, s] = both[:, a, :]
            for a, s in order:
                nc.tensor.matmul_mx(
                    out=y[a, s],
                    lhsT=ep_w[a][:, s * P : (s + 1) * P].bitcast(FP8X4),
                    lhsT_scale=e_plane[:, (2 * s + a) * P : (2 * s + a + 1) * P],
                    rhs=h_codes[:, g * P : (g + n) * P].bitcast(FP8X4),
                    rhs_scale=h_sc[c][:],
                    start=True,
                    stop=True,
                )
            for a in range(2):
                low = sb("low%d%d" % (c, a), [P, n * P], F32)
                nc.scalar.activation(low[:], y[a, 0], ACT.Identity, bias=neg_nb[:, a : a + 1])
                both = sb("pair%d%d" % (c, a), [P, n * P], F32)
                nc.vector.scalar_tensor_tensor(both[:], y[a, 1], neg_nb[:, 2 + a : 3 + a], low[:], ALU.add, ALU.max)
                for i in range(n):
                    pair[g + i, a] = both[:, i * P : (i + 1) * P]

        o_ps = {}

        def turn(g, banks):
            n = 2 // len(banks)
            o_ps[g] = []
            for i, b in enumerate(banks):
                turned = bank(b, "o_ps%d" % b, [P, n, P])
                for a in range(n):
                    nc.tensor.transpose(turned[:, a, :], pair[g, i + a], ident[:])
                o_ps[g].append((turned[:].rearrange("p a (v e) -> p (a v) e", e=2), slice(i * 64, (i + n) * 64)))

        def finish(g):
            top = sb("top%d" % g, [P, V], F32) if g >= BOTH_CLAMPED else None
            rr = sb("rr%d" % g, [P, V], F32)
            res = sb("res%d" % g, [P, V], F32)
            if g < BOTH_CLAMPED:
                two = sb("two%d" % g, [P, 2, V], F32)
                nc.scalar.activation(two[:], o_ps[g][0][0].rearrange("p v e -> p e v"), ACT.Relu, bias=own_t[:, g : g + 1], scale=-1.0)
                nc.vector.tensor_tensor(rr[:], two[:, 0, :], two[:, 1, :], ALU.min)
            for view, cols in o_ps[g] if g >= BOTH_CLAMPED else []:
                nc.vector.tensor_reduce(top[:, cols], view, mybir.AxisListType.X, ALU.max)
            if g < BOTH_CLAMPED:
                pass
            elif g < SCALAR_CLAMPS:
                nc.scalar.activation(rr[:], top[:], ACT.Relu, bias=own_t[:, g : g + 1], scale=-1.0)
            else:
                for view, cols in o_ps[g]:
                    nc.vector.tensor_scalar(rr[:, cols], top[:, cols], own_t[:, g : g + 1], 0.0, ALU.subtract, ALU.min)
            for view, cols in o_ps[g]:
                nc.scalar.activation(res[:, cols], rr[:, cols], ACT.Sqrt, bias=eps[:], scale=1.0 if g < SCALAR_CLAMPS else -1.0)
            (nc.scalar if g == GROUPS - 1 else nc.sync).dma_start(out[g * P : (g + 1) * P, :], res[:])

        gather_e(0)
        quantise(0)
        gather_e(1)
        for c in range(1, len(chunks)):
            quantise(c)
        for c in range(len(chunks)):
            product(c)
        for g in range(GROUPS):
            turn(g, [[5], [7], [0], [1, 4]][g])
        for g in range(GROUPS):
            finish(g)
